import numpy as np
import ml_dtypes


def mxq(x, axis, fmt="e4m3"):
    dtype, down = {"e4m3": (ml_dtypes.float8_e4m3fn, 7), "e5m2": (ml_dtypes.float8_e5m2, 14)}[fmt]
    v = np.moveaxis(np.asarray(x, np.float32).astype(ml_dtypes.bfloat16).astype(np.float64), axis, -1)
    blocks = v.reshape(v.shape[:-1] + (-1, 32))
    amax = np.abs(blocks).max(-1, keepdims=True)
    byte = np.maximum(np.where(amax > 0, np.frexp(amax)[1] - 1 + 127, 0) - down, 1)
    scale = np.exp2(byte - 127.0)
    codes = (blocks / scale).astype(np.float32).astype(dtype).astype(np.float64)
    return np.moveaxis((codes * scale).reshape(v.shape), -1, axis)


WIDE = False


def mx_kscale(k):
    if not WIDE:
        return np.ones(k)
    levels = np.array([10, -10, 5, -5, 0])
    if k % 512:
        return np.exp2(np.random.permutation(np.resize(levels, k // 32))).repeat(32)
    a = np.empty((k // 512, 16))
    for p in range(k // 512):
        a[p, :8] = np.random.permutation(np.resize(levels, 8))
        for g in range(8):
            far = levels[np.abs(levels - a[p, g]) >= 10]
            a[p, g + 8] = far[np.random.randint(len(far))]
    return np.exp2(a.ravel()).repeat(32)


BF16 = ml_dtypes.bfloat16


def bf(x):
    return np.asarray(x, np.float32).astype(BF16)


def f64(x):
    return np.asarray(x).astype(np.float64)


E2M1 = np.array([0.0, 0.5, 1.0, 1.5, 2.0, 3.0, 4.0, 6.0, -0.0, -0.5, -1.0, -1.5, -2.0, -3.0, -4.0, -6.0])


def pack_weight(w, fmt):
    k, n = w.shape
    w = f64(bf(w)).reshape(k // 32, 32, n)
    amax = np.abs(w).max(1)
    if fmt == "e4m3":
        byte = np.frexp(amax)[1] - 1 + 127 - 7
    else:
        mant, ex = np.frexp(amax / 6.0)
        byte = np.where(mant > 0.5, ex, ex - 1) + 127
    byte = np.clip(np.where(amax > 0, byte, 1), 1, 254)
    scaled = (w * np.exp2(127.0 - byte)[:, None, :]).reshape(k, n).astype(np.float32)
    by_word = np.ascontiguousarray(scaled.reshape(k // 512, 128, 4, n).transpose(0, 1, 3, 2))
    if fmt == "e4m3":
        words = by_word.astype(ml_dtypes.float8_e4m3fn).view(np.uint8)
    else:
        c = by_word.astype(ml_dtypes.float4_e2m1fn).view(np.uint8) & 0xF
        words = c[..., 0::2] | (c[..., 1::2] << 4)
    return np.ascontiguousarray(words), np.ascontiguousarray(byte.astype(np.uint8).reshape(k // 512, 16, n))


def unpack_weight(words, scales, fmt):
    g, p, n, _ = words.shape
    if fmt == "e4m3":
        vals = np.ascontiguousarray(words).view(ml_dtypes.float8_e4m3fn).astype(np.float64)
    else:
        nib = np.empty((g, p, n, 4), np.uint8)
        nib[..., 0::2] = words & 0xF
        nib[..., 1::2] = words >> 4
        vals = E2M1[nib]
    vals = vals * np.repeat(np.exp2(scales.astype(np.float64) - 127.0), 8, axis=1)[..., None]
    return vals.transpose(0, 1, 3, 2).reshape(g * 512, n)
def pack4(w):
    words, scales = pack_weight(w, "e2m1")
    return words.reshape(words.shape[0], 128, -1), scales


def unpack4(words, scales):
    return unpack_weight(words.reshape(words.shape[0], 128, -1, 2), scales, "e2m1")


M, E, A, N, J = 1024, 512, 1024, 2048, 512


def draw0():
    s, v = mx_kscale(E), mx_kscale(A)
    t = mx_kscale(N)
    x = np.random.standard_normal((E, M)) * s[:, None]
    y = np.random.standard_normal((E, N)) / np.sqrt(E) / s[:, None] * t
    c = np.random.standard_normal((A, M)) * v[:, None]
    d = np.random.standard_normal((A, N)) / np.sqrt(A) / v[:, None] * t
    ht = np.random.standard_normal((N, J)) / np.sqrt(N) / t[:, None]
    a = np.random.uniform(0, 1, (M, 1))
    b = np.random.uniform(0, 1, (1, N))
    d_words, d_scales = pack4(d)
    ht_words, ht_scales = pack4(ht)
    return {"x": bf(x), "y": bf(y), "c": bf(c),
            "d_words": d_words, "d_scales": d_scales,
            "taper": bf(np.exp(-3 * (a - b) ** 2)),
            "ht_words": ht_words, "ht_scales": ht_scales,
            "r": bf(1 + 0.1 * np.random.standard_normal(J))}


def core(x, y, c, d_words, d_scales, taper, ht_words, ht_scales, r):
    ens = mxq(f64(x), 0, "e4m3").T @ mxq(f64(y), 0, "e4m3")
    arc = mxq(f64(c), 0, "e4m3").T @ unpack4(d_words, d_scales)
    cov = (ens + arc) * f64(taper)
    pht = mxq(cov, 1, "e4m3") @ unpack4(ht_words, ht_scales)
    return pht * f64(r)


def e4m3fn_bytes(y):
    return np.clip(np.asarray(y, np.float64), -448.0, 448.0).astype(np.float32).astype(ml_dtypes.float8_e4m3fn).view(np.uint8)


def e4m3fn_values(b):
    return np.asarray(b, np.uint8).view(ml_dtypes.float8_e4m3fn).astype(np.float64)


def setup_inputs():
    d = draw0()
    x0 = np.asarray(d['c']).astype(np.float64)
    s = (np.max(np.abs(x0), axis=(1,), keepdims=True) / 448.0).astype(np.float32)
    out = {}
    for k, v in d.items():
        if k == 'c':
            out['c_bytes'] = e4m3fn_bytes(x0 / s.astype(np.float64))
            out['c_scale'] = s
        else:
            out[k] = v
    return out


def reference(x, y, c_bytes, c_scale, d_words, d_scales, taper, ht_words, ht_scales, r):
    return core(x, y, e4m3fn_values(c_bytes) * c_scale.astype(np.float64), d_words, d_scales, taper, ht_words, ht_scales, r)

@@ -1,0 +1,365 @@
+from contextlib import ExitStack
+
+import concourse.mybir as mybir
+from concourse.masks import make_identity
+
+M, E, A, N, J = 1024, 512, 1024, 2048, 512
+
+F32 = mybir.dt.float32
+BF16 = mybir.dt.bfloat16
+U32 = mybir.dt.uint32
+I32 = mybir.dt.int32
+U8 = mybir.dt.uint8
+FP8 = mybir.dt.float8_e4m3fn
+FP8X4 = mybir.dt.float8_e4m3fn_x4
+FP4X4 = mybir.dt.float4_e2m1fn_x4
+MULT = mybir.AluOpType.mult
+COPY = mybir.ActivationFunctionType.Copy
+
+FLOPS = 2 * M * N * (E + A + J)
+
+P = 128
+CH = 512
+NCH = N // CH
+MT = M // P
+HEAD_M = 256
+HALF = 512
+
+
+def tile_localised_covariance_observed_s3_kernel(
+    tc, x, y, c_bytes, c_scale, d_words, d_scales, taper, ht_words, ht_scales, r, out
+):
+    nc = tc.nc
+    with ExitStack() as ctx:
+        keep = ctx.enter_context(tc.tile_pool(name="keep", bufs=1))
+        stage = ctx.enter_context(tc.tile_pool(name="stage", bufs=3))
+        ps_a = ctx.enter_context(tc.psum_pool(name="ps_a", bufs=4))
+        ps_t = ctx.enter_context(tc.psum_pool(name="ps_t", bufs=1))
+        ps_o = ctx.enter_context(tc.psum_pool(name="ps_o", bufs=3))
+        ctx.enter_context(tc.manual_schedule())
+
+        def kt(shape, dtype, name):
+            return keep.tile(shape, dtype, name=name, align_bytes=64)
+
+        csc = kt([P, 2, 4], F32, "csc")
+        c_in = [kt([P, 2, 4, HALF], U8, f"c_in{h}") for h in range(2)]
+        x_in = [kt([P, 4, HALF], BF16, f"x_in{h}") for h in range(2)]
+        y_raw = [kt([P, 4, CH], BF16, f"y_raw{c}") for c in range(NCH)]
+        d_sb = [kt([P, 2, 2 * CH], U8, f"d_sb{c}") for c in range(NCH)]
+        d_sc = kt([P, 2, N], U8, "d_sc")
+        ht_sb = kt([P, 4, 2 * J], U8, "ht_sb")
+        ht_sc = kt([P, 4, J], U8, "ht_sc")
+        tap_lo = [[kt([P, 2, CH], BF16, f"tap_lo{b}{c}") for c in range(NCH)] for b in range(2)]
+        tap_hi = {mt: kt([P, N], BF16, f"tap_hi{mt}") for mt in range(4, MT)}
+        r_sb = kt([P, J], BF16, "r_sb")
+        ident = kt([P, P], F32, "ident")
+        xq = kt([P, M], U32, "xq")
+        xs = kt([P, M], U8, "xs")
+        yq = kt([P, NCH, CH], U32, "yq")
+        ys = kt([P, NCH, CH], U8, "ys")
+        cq_head = kt([P, 2, HEAD_M], U32, "cq_head")
+        cs_head = kt([P, 2, HEAD_M], U8, "cs_head")
+        cq_rest = kt([P, MT - 2, 2, P], U32, "cq_rest")
+        cs_rest = kt([P, MT - 2, 2, P], U8, "cs_rest")
+        vq = kt([P, 16, 2 * P], U32, "vq")
+        vs = kt([P, 16, 2 * P], U8, "vs")
+
+        nc.gpsimd.memset(d_sc[:].rearrange("p g n -> p (g n)").bitcast(I32), 0)
+        nc.gpsimd.memset(ht_sc[:].rearrange("p g n -> p (g n)").bitcast(I32), 0)
+        make_identity(nc, ident[:])
+
+        def load(out_, in_):
+            nc.sync.dma_start(out=out_, in_=in_)
+
+        def load_c(h):
+            for g in range(2):
+                load(c_in[h][:, g], c_bytes[512 * g : 512 * (g + 1), HALF * h : HALF * (h + 1)].rearrange("(p t) m -> p t m", t=4))
+
+        def load_x(h):
+            load(x_in[h][:], x[:, HALF * h : HALF * (h + 1)].rearrange("(p t) m -> p t m", t=4))
+
+        def load_scales(dst, src):
+            for q in range(4):
+                load(
+                    dst[32 * q : 32 * q + 4].bitcast(I32),
+                    src[:, 4 * q : 4 * q + 4, :].rearrange("g q n -> q g n").bitcast(I32),
+                )
+
+        def load_y(c):
+            load(y_raw[c][:], y[:, CH * c : CH * (c + 1)].rearrange("(p t) n -> p t n", t=4))
+
+        def load_d(c):
+            load(d_sb[c][:], d_words[:, :, 2 * CH * c : 2 * CH * (c + 1)].rearrange("g p b -> p g b"))
+
+        def load_tap(b, c):
+            load(tap_lo[b][c][:], taper[256 * b : 256 * (b + 1), CH * c : CH * (c + 1)].rearrange("(j m) n -> m j n", j=2))
+
+        load(csc[:], c_scale.rearrange("(g p t) o -> p g (t o)", p=P, t=4))
+        load_c(0)
+        load_scales(d_sc, d_scales)
+        load_d(0)
+        load_x(0)
+        load_y(0)
+        load_tap(0, 0)
+        load_d(1)
+        load_y(1)
+        load_tap(0, 1)
+        load_tap(1, 0)
+        load_tap(1, 1)
+        load_y(2)
+        load_d(2)
+        load_tap(0, 2)
+        load(ht_sb[:], ht_words.rearrange("g p b -> p g b"))
+        load_scales(ht_sc, ht_scales)
+        load_tap(1, 2)
+        load_y(3)
+        load_d(3)
+        load_tap(0, 3)
+        load_tap(1, 3)
+        load_c(1)
+        load_x(1)
+        load(r_sb[:], r.partition_broadcast(P))
+        for mt in range(4, MT):
+            load(tap_hi[mt][:], taper[P * mt : P * (mt + 1), :])
+
+        def lay(eng, dst, src):
+            d = dst.rearrange("p (c i) t -> p c t i", i=4)
+            s = src.rearrange("p t (c i) -> p c t i", i=4)
+            if eng == "v":
+                nc.vector.tensor_copy(out=d, in_=s)
+            else:
+                nc.scalar.copy(out=d, in_=s)
+
+        def quant(codes, scales, src):
+            nc.vector.quantize_mx(out=codes.bitcast(FP8X4), scales=scales, in_=src)
+
+        def widen(eng, dst, src, g):
+            for t in range(4):
+                i_ = src[:, t, :].bitcast(FP8)
+                s_ = csc[:, g, t : t + 1]
+                if eng == "v":
+                    nc.vector.tensor_scalar(out=dst[:, t, :], in0=i_, scalar1=s_, scalar2=None, op0=MULT)
+                else:
+                    nc.scalar.activation(out=dst[:, t, :], in_=i_, func=COPY, scale=s_)
+
+        y_lay = {}
+
+        def lay_y(c, splits):
+            y_lay[c] = stage.tile([P, CH, 4], BF16, name="y_lay", align_bytes=64)
+            a = 0
+            for eng, w in splits:
+                lay(eng, y_lay[c][:, a : a + w, :], y_raw[c][:, :, a : a + w])
+                a += w
+
+        def quant_y(c):
+            quant(yq[:, c, :], ys[:, c, :], y_lay[c][:].rearrange("p n t -> p (n t)"))
+
+        STEPS = [[(0, 0), (1, 0)], [(0, 1), (1, 1)], [(2, 0), (2, 1)], [(3, 0), (3, 1)]]
+        STEPS += [[(0, 2), (1, 2)], [(2, 2), (3, 2)], [(0, 3), (1, 3)], [(2, 3), (3, 3)]]
+        for mt in range(4, MT):
+            STEPS += [[(mt, 0), (mt, 1)], [(mt, 2), (mt, 3)]]
+        where = {}
+        for s, units in enumerate(STEPS):
+            for j, u in enumerate(units):
+                where[u] = (s, j)
+
+        def c_op(mt, g):
+            if mt < 2:
+                return cq_head[:, g, P * mt : P * (mt + 1)].bitcast(FP8X4), cs_head[:, g, P * mt : P * (mt + 1)]
+            return cq_rest[:, mt - 2, g, :].bitcast(FP8X4), cs_rest[:, mt - 2, g, :]
+
+        banks = {}
+
+        def cd(s):
+            for j, (mt, c) in enumerate(STEPS[s]):
+                bank = ps_a.tile([P, CH], F32, name="cov_ps")
+                banks[s, j] = bank
+                for g in range(2):
+                    lq, ls = c_op(mt, g)
+                    nc.tensor.matmul_mx(
+                        out=bank[:],
+                        lhsT=lq,
+                        lhsT_scale=ls,
+                        rhs=d_sb[c][:, g, :].bitcast(FP4X4),
+                        rhs_scale=d_sc[:, g, CH * c : CH * (c + 1)],
+                        start=(g == 0),
+                        stop=False,
+                    )
+
+        def xy(s, j):
+            mt, c = STEPS[s][j]
+            nc.tensor.matmul_mx(
+                out=banks[s, j][:],
+                lhsT=xq[:, P * mt : P * (mt + 1)].bitcast(FP8X4),
+                lhsT_scale=xs[:, P * mt : P * (mt + 1)],
+                rhs=yq[:, c, :].bitcast(FP8X4),
+                rhs_scale=ys[:, c, :],
+                start=False,
+                stop=True,
+            )
+
+        cov = {}
+
+        def taper_mul(s, j):
+            mt, c = STEPS[s][j]
+            if j == 0:
+                cov[s] = stage.tile([P, 2, CH], BF16, name="cov", align_bytes=64)
+            tp_ = tap_lo[mt // 2][c][:, mt % 2, :] if mt < 4 else tap_hi[mt][:, CH * c : CH * (c + 1)]
+            nc.vector.tensor_tensor(
+                out=cov[s][:, j, :].rearrange("m (u p e) -> m u p e", u=2, e=2),
+                in0=banks[s, j][:].rearrange("m (p u e) -> m u p e", u=2, e=2),
+                in1=tp_.rearrange("m (p u e) -> m u p e", u=2, e=2),
+                op=MULT,
+            )
+
+        turned = {}
+        grp = {}
+
+        def turn(s):
+            turned[s] = ps_t.tile([P, 2, 2, P], F32, name="turned")
+            for j in range(2):
+                for u in range(2):
+                    nc.tensor.transpose(
+                        turned[s][:, j, u, :], cov[s][:, j, 256 * u : 256 * (u + 1)].bitcast(F32), ident[:]
+                    )
+
+        def turn_out(s):
+            grp[s] = stage.tile([P, 2, P, 4], BF16, name="grp", align_bytes=64)
+            nc.scalar.copy(
+                out=grp[s][:].rearrange("p j m t -> p (j m t)").bitcast(F32).rearrange("p (j m u) -> p j m u", j=2, u=2),
+                in_=turned[s][:].rearrange("p j u m -> p j m u"),
+            )
+
+        def quant_cov(s):
+            quant(vq[:, s, :], vs[:, s, :], grp[s][:].rearrange("p j m t -> p (j m t)"))
+
+        outs = {}
+
+        def obs(mt, chunks):
+            if 0 in chunks:
+                outs[mt] = ps_o.tile([P, J], F32, name="out_ps")
+            for c in chunks:
+                s, j = where[mt, c]
+                nc.tensor.matmul_mx(
+                    out=outs[mt][:],
+                    lhsT=vq[:, s, P * j : P * (j + 1)].bitcast(FP8X4),
+                    lhsT_scale=vs[:, s, P * j : P * (j + 1)],
+                    rhs=ht_sb[:, c, :].bitcast(FP4X4),
+                    rhs_scale=ht_sc[:, c, :],
+                    start=(c == 0),
+                    stop=(c == NCH - 1),
+                )
+
+        def finish(mt):
+            res = stage.tile([P, J], F32, name="res", align_bytes=64)
+            nc.vector.tensor_tensor(out=res[:], in0=outs[mt][:], in1=r_sb[:], op=MULT)
+            nc.sync.dma_start(out=out[P * mt : P * (mt + 1), :], in_=res[:])
+
+        cw = kt([P, 2, 4, HEAD_M], BF16, "c_wide_head")
+        cl = kt([P, 2, HEAD_M, 4], BF16, "c_lay_head")
+        xl = kt([P, HEAD_M, 4], BF16, "x_lay_head")
+        widen("s", cw[:, 0], c_in[0][:, 0, :, 0:HEAD_M], 0)
+        widen("v", cw[:, 1], c_in[0][:, 1, :, 0:HEAD_M], 1)
+        lay("v", cl[:, 1], cw[:, 1])
+        lay("v", cl[:, 0], cw[:, 0])
+        for g in (1, 0):
+            quant(cq_head[:, g, :], cs_head[:, g, :], cl[:, g].rearrange("p m t -> p (m t)"))
+        lay("s", xl[:], x_in[0][:, :, 0:HEAD_M])
+        lay_y(0, [("v", 256), ("s", 256)])
+        quant(xq[:, 0:HEAD_M], xs[:, 0:HEAD_M], xl[:].rearrange("p m t -> p (m t)"))
+        quant_y(0)
+        cd(0)
+
+        wide = {}
+        laid = {}
+
+        def mt_wide(mt):
+            h, m0 = mt // 4, P * (mt % 4)
+            wide[mt] = stage.tile([P, 2, 4, P], BF16, name="c_wide", align_bytes=64)
+            for g in range(2):
+                widen("s", wide[mt][:, g], c_in[h][:, g, :, m0 : m0 + P], g)
+
+        def mt_lay_c(mt, engs):
+            laid[mt] = stage.tile([P, 2, P, 4], BF16, name="c_lay", align_bytes=64)
+            for g in range(2):
+                lay(engs[g], laid[mt][:, g], wide[mt][:, g])
+
+        def mt_lay_x(mt, eng):
+            h, m0 = mt // 4, P * (mt % 4)
+            laid[mt, "x"] = stage.tile([P, P, 4], BF16, name="x_lay", align_bytes=64)
+            lay(eng, laid[mt, "x"][:], x_in[h][:, :, m0 : m0 + P])
+
+        def mt_quant_c(mt):
+            quant(
+                cq_rest[:, mt - 2].rearrange("p g m -> p (g m)"),
+                cs_rest[:, mt - 2].rearrange("p g m -> p (g m)"),
+                laid[mt][:].rearrange("p g m t -> p (g m t)"),
+            )
+
+        def mt_quant_x(mt):
+            quant(xq[:, P * mt : P * (mt + 1)], xs[:, P * mt : P * (mt + 1)], laid[mt, "x"][:].rearrange("p m t -> p (m t)"))
+
+        def prep_y(c):
+            lay_y(c, [("v", 128), ("s", 192), ("s", 192)])
+            quant_y(c)
+
+        def prep(s):
+            if s == 0:
+                prep_y(1)
+                mt_wide(2)
+            elif s == 1:
+                mt_lay_c(2, "vv")
+                mt_lay_x(2, "s")
+                mt_quant_c(2)
+                mt_quant_x(2)
+                mt_wide(3)
+            elif s == 2:
+                mt_lay_c(3, "vv")
+                mt_lay_x(3, "s")
+                mt_quant_c(3)
+                mt_quant_x(3)
+            elif s == 3:
+                prep_y(2)
+            elif s == 4:
+                prep_y(3)
+            elif 5 <= s <= 12:
+                mt = 4 + (s - 5) // 2
+                if s % 2 == 1:
+                    mt_wide(mt)
+                else:
+                    mt_lay_c(mt, "ss")
+                    mt_lay_x(mt, "s")
+                    mt_quant_c(mt)
+                    mt_quant_x(mt)
+
+        OBS = {2: [(0, [0])], 3: [(1, [0])], 4: [(0, [1]), (1, [1])], 5: [(2, [0, 1]), (0, [2]), (1, [2])], 6: [(2, [2])], 7: [(0, [3]), (1, [3])], 8: [(2, [3]), (3, [0, 1])], 9: [(3, [2, 3])], 10: [(4, [0, 1])], 11: [(4, [2, 3])], 12: [(5, [0, 1, 2, 3])], 13: [(6, [0, 1])], 14: [(6, [2, 3])], 15: [(7, [0, 1])]}
+        TURN_FIRST = (1, 2)
+        pending = []
+        for s in range(16):
+            xy(s, 0)
+            taper_mul(s, 0)
+            if s > 0:
+                quant_cov(s - 1)
+            xy(s, 1)
+            taper_mul(s, 1)
+            for mt in pending:
+                finish(mt)
+            pending = []
+            prep(s)
+            if s in TURN_FIRST:
+                turn(s)
+                turn_out(s)
+            if s + 1 < 16:
+                cd(s + 1)
+            if s not in TURN_FIRST:
+                turn(s)
+                turn_out(s)
+            for mt, chunks in OBS.get(s, []):
+                obs(mt, chunks)
+                if 3 in chunks:
+                    pending.append(mt)
+        quant_cov(15)
+        obs(7, [2, 3])
+        for mt in pending:
+            finish(mt)
+        finish(7)

@@ -22,8 +22,315 @@ P = 128
 CH = 512
 NCH = N // CH
 MT = M // P
-HEAD_M = 256
-HALF = 512
+C_CUTS = [512,512]
+X_CUTS = [512,512]
+Y_GROUPS = [[0],[1],[2],[3]]
+D_GROUPS = [[0],[1],[2],[3]]
+T_GROUPS = [[[0],[1],[2],[3]],[[0],[1],[2],[3]]]
+
+PROGRAM = [
+    ("ld_c",0,0),
+    ("ld_csc",),
+    ("widen",2,0,"s"),
+    ("widen",3,0,"v"),
+    ("ld_c",0,1),
+    ("ld_y",0),
+    ("widen",0,0,"v"),
+    ("ld_d",0),
+    ("widen",3,1,"v"),
+    ("layc",3,0,"s"),
+    ("layc",0,0,"v"),
+    ("widen",0,1,"s"),
+    ("layy",0,1,"s"),
+    ("ld_sc","d"),
+    ("layy",0,3,"s"),
+    ("layc",2,0,"s"),
+    ("ld_x",0),
+    ("widen",2,1,"s"),
+    ("layy",0,2,"v"),
+    ("layc",0,1,"v"),
+    ("ld_y",1),
+    ("qc",0,0),
+    ("layx",2,"s"),
+    ("layy",1,2,"s"),
+    ("layy",0,0,"v"),
+    ("qc",0,1),
+    ("cd",0,0),
+    ("qy",0,2),
+    ("ld_d",1),
+    ("layy",1,0,"s"),
+    ("layx",0,"v"),
+    ("cd",0,1),
+    ("layy",1,1,"s"),
+    ("layc",3,1,"s"),
+    ("qx",0),
+    ("layc",2,1,"v"),
+    ("layy",1,3,"v"),
+    ("qc",2,2),
+    ("ld_tap",0,0),
+    ("ld_y",2),
+    ("xy",0,1),
+    ("ld_tap",0,1),
+    ("ld_c",1,1),
+    ("xy",0,0),
+    ("mul",0,0),
+    ("ld_tap",1,1),
+    ("cd",1,0),
+    ("cd",1,1),
+    ("qx",2),
+    ("cd",2,0),
+    ("ld_tap",1,0),
+    ("layx",3,"s"),
+    ("xy",2,0),
+    ("qy",1,2),
+    ("mul",0,1),
+    ("xy",1,1),
+    ("qc",3,2),
+    ("xy",1,0),
+    ("ld_d",2),
+    ("layy",2,1,"s"),
+    ("mul",1,0),
+    ("ld_d",3),
+    ("turn",0,0),
+    ("ld_c",1,0),
+    ("mul",1,1),
+    ("ld_tap",0,2),
+    ("turn",0,1),
+    ("layy",2,2,"s"),
+    ("cd",2,1),
+    ("qx",3),
+    ("xy",2,1),
+    ("ld_y",3),
+    ("layy",2,3,"s"),
+    ("cd",3,0),
+    ("layy",2,0,"v"),
+    ("widen",4,1,"s"),
+    ("mul",2,0),
+    ("cd",3,1),
+    ("ld_tap",1,2),
+    ("xy",3,0),
+    ("mul",2,1),
+    ("qy",2,2),
+    ("ld_x",1),
+    ("mul",3,0),
+    ("ld_sc","h"),
+    ("ld_ht",),
+    ("cd",4,0),
+    ("cd",4,1),
+    ("widen",4,0,"s"),
+    ("xy",3,1),
+    ("tout",0,2,"v"),
+    ("xy",4,0),
+    ("layc",4,1,"s"),
+    ("xy",4,1),
+    ("cd",5,0),
+    ("turn",1,0),
+    ("turn",1,1),
+    ("mul",3,1),
+    ("turn",2,0),
+    ("turn",2,1),
+    ("xy",5,0),
+    ("widen",6,1,"s"),
+    ("cd",5,1),
+    ("xy",5,1),
+    ("qv",0,2),
+    ("mul",4,0),
+    ("layy",3,2,"s"),
+    ("tout",1,2,"s"),
+    ("mul",4,1),
+    ("mul",5,0),
+    ("layy",3,1,"v"),
+    ("tout",2,2,"s"),
+    ("cd",6,0),
+    ("turn",3,0),
+    ("turn",3,1),
+    ("mul",5,1),
+    ("layy",3,0,"v"),
+    ("turn",4,0),
+    ("widen",5,1,"s"),
+    ("ld_tap",0,3),
+    ("qv",1,2),
+    ("layy",3,3,"s"),
+    ("qy",3,2),
+    ("turn",4,1),
+    ("layc",4,0,"v"),
+    ("widen",7,1,"s"),
+    ("cd",6,1),
+    ("cd",7,0),
+    ("layx",4,"s"),
+    ("cd",7,1),
+    ("xy",7,0),
+    ("ld_taphi",4),
+    ("layx",6,"s"),
+    ("xy",6,0),
+    ("obs",0,0),
+    ("ld_taphi",7),
+    ("obs",0,1),
+    ("layc",6,1,"v"),
+    ("widen",5,0,"s"),
+    ("tout",3,2,"s"),
+    ("xy",6,1),
+    ("layc",5,1,"s"),
+    ("xy",7,1),
+    ("qc",4,2),
+    ("ld_tap",1,3),
+    ("mul",6,0),
+    ("mul",6,1),
+    ("cd",8,0),
+    ("qx",4),
+    ("cd",8,1),
+    ("xy",8,0),
+    ("tout",4,2,"s"),
+    ("turn",5,0),
+    ("qx",6),
+    ("turn",5,1),
+    ("layx",5,"s"),
+    ("qv",2,2),
+    ("turn",6,0),
+    ("mul",7,0),
+    ("qv",3,2),
+    ("turn",6,1),
+    ("widen",6,0,"s"),
+    ("obs",1,0),
+    ("ld_taphi",5),
+    ("qv",4,2),
+    ("tout",5,2,"s"),
+    ("mul",7,1),
+    ("obs",1,1),
+    ("obs",1,2),
+    ("layc",5,0,"s"),
+    ("mul",8,0),
+    ("cd",9,0),
+    ("xy",8,1),
+    ("qc",5,2),
+    ("xy",9,0),
+    ("widen",7,0,"s"),
+    ("obs",0,2),
+    ("cd",9,1),
+    ("layc",7,1,"v"),
+    ("xy",9,1),
+    ("qx",5),
+    ("mul",8,1),
+    ("cd",10,0),
+    ("turn",7,0),
+    ("turn",7,1),
+    ("tout",6,2,"s"),
+    ("turn",8,0),
+    ("mul",9,0),
+    ("turn",8,1),
+    ("ld_r",),
+    ("qv",6,2),
+    ("obs",0,3),
+    ("ld_taphi",6),
+    ("tout",7,2,"s"),
+    ("layc",6,0,"v"),
+    ("obs",1,3),
+    ("xy",10,0),
+    ("cd",10,1),
+    ("layc",7,0,"v"),
+    ("qc",6,2),
+    ("xy",10,1),
+    ("cd",11,0),
+    ("qc",7,2),
+    ("mul",9,1),
+    ("xy",11,0),
+    ("cd",11,1),
+    ("mul",10,0),
+    ("cd",12,0),
+    ("mul",10,1),
+    ("mul",11,0),
+    ("xy",11,1),
+    ("qv",5,2),
+    ("fin",0,2),
+    ("cd",12,1),
+    ("qv",7,2),
+    ("turn",9,0),
+    ("tout",8,2,"s"),
+    ("turn",9,1),
+    ("turn",10,0),
+    ("mul",11,1),
+    ("fin",1,2),
+    ("turn",10,1),
+    ("xy",12,0),
+    ("xy",12,1),
+    ("tout",9,2,"s"),
+    ("cd",13,0),
+    ("cd",13,1),
+    ("obs",2,0),
+    ("obs",2,1),
+    ("layx",7,"v"),
+    ("obs",3,0),
+    ("tout",10,2,"v"),
+    ("qx",7),
+    ("xy",13,1),
+    ("mul",12,0),
+    ("cd",14,0),
+    ("mul",12,1),
+    ("turn",11,0),
+    ("turn",11,1),
+    ("turn",12,0),
+    ("turn",12,1),
+    ("xy",13,0),
+    ("qv",9,2),
+    ("obs",3,1),
+    ("obs",3,2),
+    ("qv",8,2),
+    ("cd",14,1),
+    ("tout",11,2,"s"),
+    ("qv",11,2),
+    ("obs",2,2),
+    ("qv",10,2),
+    ("mul",13,0),
+    ("mul",13,1),
+    ("obs",2,3),
+    ("obs",3,3),
+    ("fin",2,2),
+    ("xy",14,0),
+    ("xy",14,1),
+    ("cd",15,0),
+    ("tout",12,2,"s"),
+    ("xy",15,0),
+    ("fin",3,2),
+    ("mul",14,0),
+    ("obs",4,0),
+    ("mul",14,1),
+    ("obs",4,1),
+    ("cd",15,1),
+    ("obs",4,2),
+    ("xy",15,1),
+    ("obs",4,3),
+    ("turn",13,0),
+    ("mul",15,0),
+    ("turn",13,1),
+    ("turn",14,0),
+    ("fin",4,2),
+    ("mul",15,1),
+    ("turn",14,1),
+    ("tout",13,2,"s"),
+    ("obs",5,0),
+    ("tout",14,2,"s"),
+    ("qv",12,2),
+    ("obs",5,1),
+    ("qv",14,2),
+    ("turn",15,0),
+    ("turn",15,1),
+    ("obs",5,2),
+    ("obs",5,3),
+    ("qv",13,2),
+    ("obs",6,0),
+    ("tout",15,2,"s"),
+    ("qv",15,2),
+    ("fin",5,2),
+    ("obs",6,1),
+    ("obs",6,2),
+    ("obs",6,3),
+    ("obs",7,0),
+    ("obs",7,1),
+    ("obs",7,2),
+    ("obs",7,3),
+    ("fin",6,2),
+    ("fin",7,2),
+]
 
 
 def tile_localised_covariance_observed_s3_kernel(
@@ -32,24 +339,31 @@ def tile_localised_covariance_observed_s3_kernel(
     nc = tc.nc
     with ExitStack() as ctx:
         keep = ctx.enter_context(tc.tile_pool(name="keep", bufs=1))
-        stage = ctx.enter_context(tc.tile_pool(name="stage", bufs=3))
+        covp = ctx.enter_context(tc.tile_pool(name="covp", bufs=4))
+        grpp = ctx.enter_context(tc.tile_pool(name="grpp", bufs=3))
+        resp = ctx.enter_context(tc.tile_pool(name="resp", bufs=3))
         ps_a = ctx.enter_context(tc.psum_pool(name="ps_a", bufs=4))
-        ps_t = ctx.enter_context(tc.psum_pool(name="ps_t", bufs=1))
-        ps_o = ctx.enter_context(tc.psum_pool(name="ps_o", bufs=3))
+        ps_t = ctx.enter_context(tc.psum_pool(name="ps_t", bufs=2))
+        ps_o = ctx.enter_context(tc.psum_pool(name="ps_o", bufs=2))
         ctx.enter_context(tc.manual_schedule())
 
         def kt(shape, dtype, name):
             return keep.tile(shape, dtype, name=name, align_bytes=64)
 
+        c_starts = [sum(C_CUTS[:k]) for k in range(len(C_CUTS))]
+        x_starts = [sum(X_CUTS[:k]) for k in range(len(X_CUTS))]
         csc = kt([P, 2, 4], F32, "csc")
-        c_in = [kt([P, 2, 4, HALF], U8, f"c_in{h}") for h in range(2)]
-        x_in = [kt([P, 4, HALF], BF16, f"x_in{h}") for h in range(2)]
-        y_raw = [kt([P, 4, CH], BF16, f"y_raw{c}") for c in range(NCH)]
-        d_sb = [kt([P, 2, 2 * CH], U8, f"d_sb{c}") for c in range(NCH)]
+        c_in = [kt([P, 2, 4, w], U8, f"c_in{k}") for k, w in enumerate(C_CUTS)]
+        x_in = [kt([P, 4, w], BF16, f"x_in{k}") for k, w in enumerate(X_CUTS)]
+        y_grp = [kt([P, 4, CH * len(g)], BF16, f"y_in{k}") for k, g in enumerate(Y_GROUPS)]
+        y_in = {c: y_grp[k][:, :, CH * i : CH * (i + 1)] for k, g in enumerate(Y_GROUPS) for i, c in enumerate(g)}
+        d_grp = [kt([P, 2, 2 * CH * len(g)], U8, f"d_sb{k}") for k, g in enumerate(D_GROUPS)]
+        d_sb = {c: d_grp[k][:, :, 2 * CH * i : 2 * CH * (i + 1)] for k, g in enumerate(D_GROUPS) for i, c in enumerate(g)}
         d_sc = kt([P, 2, N], U8, "d_sc")
         ht_sb = kt([P, 4, 2 * J], U8, "ht_sb")
         ht_sc = kt([P, 4, J], U8, "ht_sc")
-        tap_lo = [[kt([P, 2, CH], BF16, f"tap_lo{b}{c}") for c in range(NCH)] for b in range(2)]
+        t_grp = [[kt([P, 2, CH * len(g)], BF16, f"tap_lo{b}{k}") for k, g in enumerate(T_GROUPS[b])] for b in range(2)]
+        tap_lo = [{c: t_grp[b][k][:, :, CH * i : CH * (i + 1)] for k, g in enumerate(T_GROUPS[b]) for i, c in enumerate(g)} for b in range(2)]
         tap_hi = {mt: kt([P, N], BF16, f"tap_hi{mt}") for mt in range(4, MT)}
         r_sb = kt([P, J], BF16, "r_sb")
         ident = kt([P, P], F32, "ident")
@@ -57,12 +371,15 @@ def tile_localised_covariance_observed_s3_kernel(
         xs = kt([P, M], U8, "xs")
         yq = kt([P, NCH, CH], U32, "yq")
         ys = kt([P, NCH, CH], U8, "ys")
-        cq_head = kt([P, 2, HEAD_M], U32, "cq_head")
-        cs_head = kt([P, 2, HEAD_M], U8, "cs_head")
-        cq_rest = kt([P, MT - 2, 2, P], U32, "cq_rest")
-        cs_rest = kt([P, MT - 2, 2, P], U8, "cs_rest")
         vq = kt([P, 16, 2 * P], U32, "vq")
         vs = kt([P, 16, 2 * P], U8, "vs")
+        BLOCKS = {0: (0, 256), 2: (256, 128), 3: (384, 128), 4: (512, 128), 5: (640, 128), 6: (768, 128), 7: (896, 128)}
+        cq = {b: kt([P, 2, w], U32, f"cq{b}") for b, (m0, w) in BLOCKS.items()}
+        cs = {b: kt([P, 2, w], U8, f"cs{b}") for b, (m0, w) in BLOCKS.items()}
+        c_wide = {b: kt([P, 2, 4, w], BF16, f"c_wide{b}") for b, (m0, w) in BLOCKS.items()}
+        c_lay = {b: kt([P, 2, w, 4], BF16, f"c_lay{b}") for b, (m0, w) in BLOCKS.items()}
+        x_lay = {b: kt([P, w, 4], BF16, f"x_lay{b}") for b, (m0, w) in BLOCKS.items()}
+        y_lay = [kt([P, CH, 4], BF16, f"y_lay{c}") for c in range(NCH)]
 
         nc.gpsimd.memset(d_sc[:].rearrange("p g n -> p (g n)").bitcast(I32), 0)
         nc.gpsimd.memset(ht_sc[:].rearrange("p g n -> p (g n)").bitcast(I32), 0)
@@ -71,56 +388,49 @@ def tile_localised_covariance_observed_s3_kernel(
         def load(out_, in_):
             nc.sync.dma_start(out=out_, in_=in_)
 
-        def load_c(h):
-            for g in range(2):
-                load(c_in[h][:, g], c_bytes[512 * g : 512 * (g + 1), HALF * h : HALF * (h + 1)].rearrange("(p t) m -> p t m", t=4))
+        def ld_csc():
+            load(csc[:], c_scale.rearrange("(g p t) o -> p g (t o)", p=P, t=4))
 
-        def load_x(h):
-            load(x_in[h][:], x[:, HALF * h : HALF * (h + 1)].rearrange("(p t) m -> p t m", t=4))
+        def ld_c(k, g):
+            m0, w = c_starts[k], C_CUTS[k]
+            load(c_in[k][:, g], c_bytes[512 * g : 512 * (g + 1), m0 : m0 + w].rearrange("(p t) m -> p t m", t=4))
 
-        def load_scales(dst, src):
+        def ld_x(k):
+            m0, w = x_starts[k], X_CUTS[k]
+            load(x_in[k][:], x[:, m0 : m0 + w].rearrange("(p t) m -> p t m", t=4))
+
+        def ld_sc(which):
+            dst, src = (d_sc, d_scales) if which == "d" else (ht_sc, ht_scales)
             for q in range(4):
                 load(
                     dst[32 * q : 32 * q + 4].bitcast(I32),
                     src[:, 4 * q : 4 * q + 4, :].rearrange("g q n -> q g n").bitcast(I32),
                 )
 
-        def load_y(c):
-            load(y_raw[c][:], y[:, CH * c : CH * (c + 1)].rearrange("(p t) n -> p t n", t=4))
+        def ld_y(k):
+            n0, w = CH * Y_GROUPS[k][0], CH * len(Y_GROUPS[k])
+            load(y_grp[k][:], y[:, n0 : n0 + w].rearrange("(p t) n -> p t n", t=4))
 
-        def load_d(c):
-            load(d_sb[c][:], d_words[:, :, 2 * CH * c : 2 * CH * (c + 1)].rearrange("g p b -> p g b"))
+        def ld_d(k):
+            n0, w = 2 * CH * D_GROUPS[k][0], 2 * CH * len(D_GROUPS[k])
+            load(d_grp[k][:], d_words[:, :, n0 : n0 + w].rearrange("g p b -> p g b"))
 
-        def load_tap(b, c):
-            load(tap_lo[b][c][:], taper[256 * b : 256 * (b + 1), CH * c : CH * (c + 1)].rearrange("(j m) n -> m j n", j=2))
+        def ld_tap(b, k):
+            n0, w = CH * T_GROUPS[b][k][0], CH * len(T_GROUPS[b][k])
+            load(t_grp[b][k][:], taper[256 * b : 256 * (b + 1), n0 : n0 + w].rearrange("(j m) n -> m j n", j=2))
 
-        load(csc[:], c_scale.rearrange("(g p t) o -> p g (t o)", p=P, t=4))
-        load_c(0)
-        load_scales(d_sc, d_scales)
-        load_d(0)
-        load_x(0)
-        load_y(0)
-        load_tap(0, 0)
-        load_d(1)
-        load_y(1)
-        load_tap(0, 1)
-        load_tap(1, 0)
-        load_tap(1, 1)
-        load_y(2)
-        load_d(2)
-        load_tap(0, 2)
-        load(ht_sb[:], ht_words.rearrange("g p b -> p g b"))
-        load_scales(ht_sc, ht_scales)
-        load_tap(1, 2)
-        load_y(3)
-        load_d(3)
-        load_tap(0, 3)
-        load_tap(1, 3)
-        load_c(1)
-        load_x(1)
-        load(r_sb[:], r.partition_broadcast(P))
-        for mt in range(4, MT):
+        def ld_taphi(mt):
             load(tap_hi[mt][:], taper[P * mt : P * (mt + 1), :])
+
+        def ld_ht():
+            load(ht_sb[:], ht_words.rearrange("g p b -> p g b"))
+
+        def ld_r():
+            load(r_sb[:], r.partition_broadcast(P))
+
+        def cut(starts, m0):
+            k = max(i for i in range(len(starts)) if starts[i] <= m0)
+            return k, m0 - starts[k]
 
         def lay(eng, dst, src):
             d = dst.rearrange("p (c i) t -> p c t i", i=4)
@@ -133,29 +443,51 @@ def tile_localised_covariance_observed_s3_kernel(
         def quant(codes, scales, src):
             nc.vector.quantize_mx(out=codes.bitcast(FP8X4), scales=scales, in_=src)
 
-        def widen(eng, dst, src, g):
+        def widen(b, g, eng):
+            m0, w = BLOCKS[b]
+            k, a = cut(c_starts, m0)
             for t in range(4):
-                i_ = src[:, t, :].bitcast(FP8)
+                i_ = c_in[k][:, g, t, a : a + w].bitcast(FP8)
                 s_ = csc[:, g, t : t + 1]
+                o_ = c_wide[b][:, g, t, :]
                 if eng == "v":
-                    nc.vector.tensor_scalar(out=dst[:, t, :], in0=i_, scalar1=s_, scalar2=None, op0=MULT)
+                    nc.vector.tensor_scalar(out=o_, in0=i_, scalar1=s_, scalar2=None, op0=MULT)
                 else:
-                    nc.scalar.activation(out=dst[:, t, :], in_=i_, func=COPY, scale=s_)
+                    nc.scalar.activation(out=o_, in_=i_, func=COPY, scale=s_)
 
-        y_lay = {}
+        def layc(b, g, eng):
+            lay(eng, c_lay[b][:, g], c_wide[b][:, g])
 
-        def lay_y(c, splits):
-            y_lay[c] = stage.tile([P, CH, 4], BF16, name="y_lay", align_bytes=64)
-            a = 0
-            for eng, w in splits:
-                lay(eng, y_lay[c][:, a : a + w, :], y_raw[c][:, :, a : a + w])
-                a += w
+        def layx(b, eng):
+            m0, w = BLOCKS[b]
+            k, a = cut(x_starts, m0)
+            lay(eng, x_lay[b][:], x_in[k][:, :, a : a + w])
 
-        def quant_y(c):
-            quant(yq[:, c, :], ys[:, c, :], y_lay[c][:].rearrange("p n t -> p (n t)"))
+        def layy(c, i, eng):
+            lay(eng, y_lay[c][:, 128 * i : 128 * (i + 1), :], y_in[c][:, :, 128 * i : 128 * (i + 1)])
 
-        STEPS = [[(0, 0), (1, 0)], [(0, 1), (1, 1)], [(2, 0), (2, 1)], [(3, 0), (3, 1)]]
-        STEPS += [[(0, 2), (1, 2)], [(2, 2), (3, 2)], [(0, 3), (1, 3)], [(2, 3), (3, 3)]]
+        def qc(b, g):
+            if g < 2:
+                quant(cq[b][:, g, :], cs[b][:, g, :], c_lay[b][:, g].rearrange("p m t -> p (m t)"))
+            else:
+                quant(
+                    cq[b][:].rearrange("p g m -> p (g m)"),
+                    cs[b][:].rearrange("p g m -> p (g m)"),
+                    c_lay[b][:].rearrange("p g m t -> p (g m t)"),
+                )
+
+        def qx(b):
+            m0, w = BLOCKS[b]
+            quant(xq[:, m0 : m0 + w], xs[:, m0 : m0 + w], x_lay[b][:].rearrange("p m t -> p (m t)"))
+
+        def qy(c, half):
+            if half < 2:
+                n0 = 256 * half
+                quant(yq[:, c, n0 : n0 + 256], ys[:, c, n0 : n0 + 256], y_lay[c][:, n0 : n0 + 256].rearrange("p n t -> p (n t)"))
+            else:
+                quant(yq[:, c, :], ys[:, c, :], y_lay[c][:].rearrange("p n t -> p (n t)"))
+
+        STEPS = [[(0, 0), (1, 0)], [(0, 1), (1, 1)], [(2, 0), (2, 1)], [(3, 0), (3, 1)], [(0, 2), (1, 2)], [(2, 2), (3, 2)], [(0, 3), (1, 3)], [(2, 3), (3, 3)]]
         for mt in range(4, MT):
             STEPS += [[(mt, 0), (mt, 1)], [(mt, 2), (mt, 3)]]
         where = {}
@@ -163,28 +495,24 @@ def tile_localised_covariance_observed_s3_kernel(
             for j, u in enumerate(units):
                 where[u] = (s, j)
 
-        def c_op(mt, g):
-            if mt < 2:
-                return cq_head[:, g, P * mt : P * (mt + 1)].bitcast(FP8X4), cs_head[:, g, P * mt : P * (mt + 1)]
-            return cq_rest[:, mt - 2, g, :].bitcast(FP8X4), cs_rest[:, mt - 2, g, :]
-
         banks = {}
 
-        def cd(s):
-            for j, (mt, c) in enumerate(STEPS[s]):
-                bank = ps_a.tile([P, CH], F32, name="cov_ps")
-                banks[s, j] = bank
-                for g in range(2):
-                    lq, ls = c_op(mt, g)
-                    nc.tensor.matmul_mx(
-                        out=bank[:],
-                        lhsT=lq,
-                        lhsT_scale=ls,
-                        rhs=d_sb[c][:, g, :].bitcast(FP4X4),
-                        rhs_scale=d_sc[:, g, CH * c : CH * (c + 1)],
-                        start=(g == 0),
-                        stop=False,
-                    )
+        def cd(s, j):
+            mt, c = STEPS[s][j]
+            b = 0 if mt < 2 else mt
+            a = P * mt if mt < 2 else 0
+            bank = ps_a.tile([P, CH], F32, name="cov_ps")
+            banks[s, j] = bank
+            for g in range(2):
+                nc.tensor.matmul_mx(
+                    out=bank[:],
+                    lhsT=cq[b][:, g, a : a + P].bitcast(FP8X4),
+                    lhsT_scale=cs[b][:, g, a : a + P],
+                    rhs=d_sb[c][:, g, :].bitcast(FP4X4),
+                    rhs_scale=d_sc[:, g, CH * c : CH * (c + 1)],
+                    start=(g == 0),
+                    stop=False,
+                )
 
         def xy(s, j):
             mt, c = STEPS[s][j]
@@ -200,10 +528,10 @@ def tile_localised_covariance_observed_s3_kernel(
 
         cov = {}
 
-        def taper_mul(s, j):
+        def mul(s, j):
             mt, c = STEPS[s][j]
-            if j == 0:
-                cov[s] = stage.tile([P, 2, CH], BF16, name="cov", align_bytes=64)
+            if s not in cov:
+                cov[s] = covp.tile([P, 2, CH], BF16, name="cov", align_bytes=64)
             tp_ = tap_lo[mt // 2][c][:, mt % 2, :] if mt < 4 else tap_hi[mt][:, CH * c : CH * (c + 1)]
             nc.vector.tensor_tensor(
                 out=cov[s][:, j, :].rearrange("m (u p e) -> m u p e", u=2, e=2),
@@ -215,151 +543,69 @@ def tile_localised_covariance_observed_s3_kernel(
         turned = {}
         grp = {}
 
-        def turn(s):
-            turned[s] = ps_t.tile([P, 2, 2, P], F32, name="turned")
-            for j in range(2):
-                for u in range(2):
-                    nc.tensor.transpose(
-                        turned[s][:, j, u, :], cov[s][:, j, 256 * u : 256 * (u + 1)].bitcast(F32), ident[:]
-                    )
+        def turn(s, j):
+            if s not in turned:
+                turned[s] = ps_t.tile([P, 2, 2, P], F32, name="turned")
+            for u in range(2):
+                nc.tensor.transpose(
+                    turned[s][:, j, u, :], cov[s][:, j, 256 * u : 256 * (u + 1)].bitcast(F32), ident[:]
+                )
 
-        def turn_out(s):
-            grp[s] = stage.tile([P, 2, P, 4], BF16, name="grp", align_bytes=64)
-            nc.scalar.copy(
-                out=grp[s][:].rearrange("p j m t -> p (j m t)").bitcast(F32).rearrange("p (j m u) -> p j m u", j=2, u=2),
-                in_=turned[s][:].rearrange("p j u m -> p j m u"),
-            )
+        def tout(s, j, eng):
+            if s not in grp:
+                grp[s] = grpp.tile([P, 2, P, 4], BF16, name="grp", align_bytes=64)
+            if j < 2:
+                o_ = grp[s][:, j].rearrange("p m t -> p (m t)").bitcast(F32).rearrange("p (m u) -> p m u", u=2)
+                i_ = turned[s][:, j].rearrange("p u m -> p m u")
+            else:
+                o_ = grp[s][:].rearrange("p j m t -> p (j m t)").bitcast(F32).rearrange("p (j m u) -> p j m u", j=2, u=2)
+                i_ = turned[s][:].rearrange("p j u m -> p j m u")
+            if eng == "v":
+                nc.vector.tensor_copy(out=o_, in_=i_)
+            else:
+                nc.scalar.copy(out=o_, in_=i_)
 
-        def quant_cov(s):
-            quant(vq[:, s, :], vs[:, s, :], grp[s][:].rearrange("p j m t -> p (j m t)"))
+        def qv(s, j):
+            if j < 2:
+                quant(vq[:, s, P * j : P * (j + 1)], vs[:, s, P * j : P * (j + 1)], grp[s][:, j].rearrange("p m t -> p (m t)"))
+            else:
+                quant(vq[:, s, :], vs[:, s, :], grp[s][:].rearrange("p j m t -> p (j m t)"))
 
         outs = {}
 
-        def obs(mt, chunks):
-            if 0 in chunks:
+        def obs(mt, c):
+            if mt not in outs:
                 outs[mt] = ps_o.tile([P, J], F32, name="out_ps")
-            for c in chunks:
-                s, j = where[mt, c]
-                nc.tensor.matmul_mx(
-                    out=outs[mt][:],
-                    lhsT=vq[:, s, P * j : P * (j + 1)].bitcast(FP8X4),
-                    lhsT_scale=vs[:, s, P * j : P * (j + 1)],
-                    rhs=ht_sb[:, c, :].bitcast(FP4X4),
-                    rhs_scale=ht_sc[:, c, :],
-                    start=(c == 0),
-                    stop=(c == NCH - 1),
-                )
-
-        def finish(mt):
-            res = stage.tile([P, J], F32, name="res", align_bytes=64)
-            nc.vector.tensor_tensor(out=res[:], in0=outs[mt][:], in1=r_sb[:], op=MULT)
-            nc.sync.dma_start(out=out[P * mt : P * (mt + 1), :], in_=res[:])
-
-        cw = kt([P, 2, 4, HEAD_M], BF16, "c_wide_head")
-        cl = kt([P, 2, HEAD_M, 4], BF16, "c_lay_head")
-        xl = kt([P, HEAD_M, 4], BF16, "x_lay_head")
-        widen("s", cw[:, 0], c_in[0][:, 0, :, 0:HEAD_M], 0)
-        widen("v", cw[:, 1], c_in[0][:, 1, :, 0:HEAD_M], 1)
-        lay("v", cl[:, 1], cw[:, 1])
-        lay("v", cl[:, 0], cw[:, 0])
-        for g in (1, 0):
-            quant(cq_head[:, g, :], cs_head[:, g, :], cl[:, g].rearrange("p m t -> p (m t)"))
-        lay("s", xl[:], x_in[0][:, :, 0:HEAD_M])
-        lay_y(0, [("v", 256), ("s", 256)])
-        quant(xq[:, 0:HEAD_M], xs[:, 0:HEAD_M], xl[:].rearrange("p m t -> p (m t)"))
-        quant_y(0)
-        cd(0)
-
-        wide = {}
-        laid = {}
-
-        def mt_wide(mt):
-            h, m0 = mt // 4, P * (mt % 4)
-            wide[mt] = stage.tile([P, 2, 4, P], BF16, name="c_wide", align_bytes=64)
-            for g in range(2):
-                widen("s", wide[mt][:, g], c_in[h][:, g, :, m0 : m0 + P], g)
-
-        def mt_lay_c(mt, engs):
-            laid[mt] = stage.tile([P, 2, P, 4], BF16, name="c_lay", align_bytes=64)
-            for g in range(2):
-                lay(engs[g], laid[mt][:, g], wide[mt][:, g])
-
-        def mt_lay_x(mt, eng):
-            h, m0 = mt // 4, P * (mt % 4)
-            laid[mt, "x"] = stage.tile([P, P, 4], BF16, name="x_lay", align_bytes=64)
-            lay(eng, laid[mt, "x"][:], x_in[h][:, :, m0 : m0 + P])
-
-        def mt_quant_c(mt):
-            quant(
-                cq_rest[:, mt - 2].rearrange("p g m -> p (g m)"),
-                cs_rest[:, mt - 2].rearrange("p g m -> p (g m)"),
-                laid[mt][:].rearrange("p g m t -> p (g m t)"),
+            s, j = where[mt, c]
+            nc.tensor.matmul_mx(
+                out=outs[mt][:],
+                lhsT=vq[:, s, P * j : P * (j + 1)].bitcast(FP8X4),
+                lhsT_scale=vs[:, s, P * j : P * (j + 1)],
+                rhs=ht_sb[:, c, :].bitcast(FP4X4),
+                rhs_scale=ht_sc[:, c, :],
+                start=(c == 0),
+                stop=(c == NCH - 1),
             )
 
-        def mt_quant_x(mt):
-            quant(xq[:, P * mt : P * (mt + 1)], xs[:, P * mt : P * (mt + 1)], laid[mt, "x"][:].rearrange("p m t -> p (m t)"))
+        res = {}
 
-        def prep_y(c):
-            lay_y(c, [("v", 128), ("s", 192), ("s", 192)])
-            quant_y(c)
+        def fin(mt, h):
+            if h == 2:
+                res[mt] = resp.tile([P, J], F32, name="res", align_bytes=64)
+                nc.vector.tensor_tensor(out=res[mt][:], in0=outs[mt][:], in1=r_sb[:], op=MULT)
+                nc.sync.dma_start(out=out[P * mt : P * (mt + 1), :], in_=res[mt][:])
+            else:
+                if mt not in res:
+                    res[mt] = resp.tile([P, J], F32, name="res", align_bytes=64)
+                cols = slice(256 * h, 256 * (h + 1))
+                nc.vector.tensor_tensor(out=res[mt][:, cols], in0=outs[mt][:, cols], in1=r_sb[:, cols], op=MULT)
+                nc.sync.dma_start(out=out[P * mt : P * (mt + 1), cols], in_=res[mt][:, cols])
 
-        def prep(s):
-            if s == 0:
-                prep_y(1)
-                mt_wide(2)
-            elif s == 1:
-                mt_lay_c(2, "vv")
-                mt_lay_x(2, "s")
-                mt_quant_c(2)
-                mt_quant_x(2)
-                mt_wide(3)
-            elif s == 2:
-                mt_lay_c(3, "vv")
-                mt_lay_x(3, "s")
-                mt_quant_c(3)
-                mt_quant_x(3)
-            elif s == 3:
-                prep_y(2)
-            elif s == 4:
-                prep_y(3)
-            elif 5 <= s <= 12:
-                mt = 4 + (s - 5) // 2
-                if s % 2 == 1:
-                    mt_wide(mt)
-                else:
-                    mt_lay_c(mt, "ss")
-                    mt_lay_x(mt, "s")
-                    mt_quant_c(mt)
-                    mt_quant_x(mt)
-
-        OBS = {2: [(0, [0])], 3: [(1, [0])], 4: [(0, [1]), (1, [1])], 5: [(2, [0, 1]), (0, [2]), (1, [2])], 6: [(2, [2])], 7: [(0, [3]), (1, [3])], 8: [(2, [3]), (3, [0, 1])], 9: [(3, [2, 3])], 10: [(4, [0, 1])], 11: [(4, [2, 3])], 12: [(5, [0, 1, 2, 3])], 13: [(6, [0, 1])], 14: [(6, [2, 3])], 15: [(7, [0, 1])]}
-        TURN_FIRST = (1, 2)
-        pending = []
-        for s in range(16):
-            xy(s, 0)
-            taper_mul(s, 0)
-            if s > 0:
-                quant_cov(s - 1)
-            xy(s, 1)
-            taper_mul(s, 1)
-            for mt in pending:
-                finish(mt)
-            pending = []
-            prep(s)
-            if s in TURN_FIRST:
-                turn(s)
-                turn_out(s)
-            if s + 1 < 16:
-                cd(s + 1)
-            if s not in TURN_FIRST:
-                turn(s)
-                turn_out(s)
-            for mt, chunks in OBS.get(s, []):
-                obs(mt, chunks)
-                if 3 in chunks:
-                    pending.append(mt)
-        quant_cov(15)
-        obs(7, [2, 3])
-        for mt in pending:
-            finish(mt)
-        finish(7)
+        calls = {
+            "ld_csc": ld_csc, "ld_c": ld_c, "ld_x": ld_x, "ld_sc": ld_sc, "ld_y": ld_y, "ld_d": ld_d, "ld_tap": ld_tap,
+            "ld_taphi": ld_taphi, "ld_ht": ld_ht, "ld_r": ld_r, "widen": widen, "layc": layc, "layx": layx, "layy": layy,
+            "qc": qc, "qx": qx, "qy": qy, "cd": cd, "xy": xy, "mul": mul, "turn": turn, "tout": tout, "qv": qv,
+            "obs": obs, "fin": fin,
+        }
+        for item in PROGRAM:
+            calls[item[0]](*item[1:])

@@ -22,314 +22,319 @@ P = 128
 CH = 512
 NCH = N // CH
 MT = M // P
-C_CUTS = [512,512]
-X_CUTS = [512,512]
+C_CUTS = [256,256,512]
+X_CUTS = [256,256,512]
 Y_GROUPS = [[0],[1],[2],[3]]
 D_GROUPS = [[0],[1],[2],[3]]
 T_GROUPS = [[[0],[1],[2],[3]],[[0],[1],[2],[3]]]
 
 PROGRAM = [
-    ("ld_c",0,0),
-    ("ld_csc",),
-    ("widen",2,0,"s"),
-    ("widen",3,0,"v"),
-    ("ld_c",0,1),
-    ("ld_y",0),
-    ("widen",0,0,"v"),
-    ("ld_d",0),
-    ("widen",3,1,"v"),
-    ("layc",3,0,"s"),
-    ("layc",0,0,"v"),
-    ("widen",0,1,"s"),
-    ("layy",0,1,"s"),
-    ("ld_sc","d"),
-    ("layy",0,3,"s"),
-    ("layc",2,0,"s"),
-    ("ld_x",0),
-    ("widen",2,1,"s"),
-    ("layy",0,2,"v"),
-    ("layc",0,1,"v"),
-    ("ld_y",1),
-    ("qc",0,0),
-    ("layx",2,"s"),
-    ("layy",1,2,"s"),
-    ("layy",0,0,"v"),
-    ("qc",0,1),
-    ("cd",0,0),
-    ("qy",0,2),
-    ("ld_d",1),
-    ("layy",1,0,"s"),
-    ("layx",0,"v"),
-    ("cd",0,1),
-    ("layy",1,1,"s"),
-    ("layc",3,1,"s"),
-    ("qx",0),
-    ("layc",2,1,"v"),
-    ("layy",1,3,"v"),
-    ("qc",2,2),
-    ("ld_tap",0,0),
-    ("ld_y",2),
-    ("xy",0,1),
-    ("ld_tap",0,1),
-    ("ld_c",1,1),
-    ("xy",0,0),
-    ("mul",0,0),
-    ("ld_tap",1,1),
-    ("cd",1,0),
-    ("cd",1,1),
-    ("qx",2),
-    ("cd",2,0),
-    ("ld_tap",1,0),
-    ("layx",3,"s"),
-    ("xy",2,0),
-    ("qy",1,2),
-    ("mul",0,1),
-    ("xy",1,1),
-    ("qc",3,2),
-    ("xy",1,0),
-    ("ld_d",2),
-    ("layy",2,1,"s"),
-    ("mul",1,0),
-    ("ld_d",3),
-    ("turn",0,0),
     ("ld_c",1,0),
-    ("mul",1,1),
-    ("ld_tap",0,2),
-    ("turn",0,1),
-    ("layy",2,2,"s"),
-    ("cd",2,1),
-    ("qx",3),
-    ("xy",2,1),
-    ("ld_y",3),
-    ("layy",2,3,"s"),
-    ("cd",3,0),
-    ("layy",2,0,"v"),
-    ("widen",4,1,"s"),
-    ("mul",2,0),
-    ("cd",3,1),
-    ("ld_tap",1,2),
-    ("xy",3,0),
-    ("mul",2,1),
-    ("qy",2,2),
+    ("ld_csc",),
+    ("widen",2,0,"v"),
+    ("ld_c",0,1),
+    ("widen",3,0,"s"),
+    ("ld_c",0,0),
+    ("widen",0,1,"v"),
+    ("ld_c",1,1),
+    ("layc",2,0,"s"),
+    ("ld_y",0),
+    ("ld_sc","d"),
+    ("widen",0,0,"v"),
+    ("layc",0,1,"v"),
+    ("ld_d",0),
+    ("widen",3,1,"s"),
+    ("widen",2,1,"s"),
+    ("ld_d",1),
+    ("layy",0,0,"s"),
+    ("layc",0,0,"v"),
+    ("qc",0,1),
+    ("qc",0,0),
     ("ld_x",1),
-    ("mul",3,0),
-    ("ld_sc","h"),
+    ("layy",0,2,"v"),
+    ("warm",2),
+    ("layy",0,1,"v"),
+    ("layc",3,1,"v"),
+    ("layc",2,1,"s"),
+    ("layc",3,0,"s"),
+    ("ld_x",0),
+    ("ld_y",1),
+    ("layy",0,3,"s"),
+    ("ld_tap",0,0),
+    ("cd",0,0),
+    ("layx",3,"s"),
+    ("qc",2,2),
+    ("qc",3,2),
+    ("layx",0,"s"),
+    ("layx",2,"v"),
+    ("qx",3),
+    ("ld_y",2),
+    ("ld_tap",0,1),
+    ("qx",2),
+    ("cd",0,1),
+    ("ld_d",2),
+    ("qy",0,2),
+    ("layy",1,2,"s"),
+    ("cd",1,0),
+    ("qx",0),
+    ("cd",1,1),
+    ("ld_tap",1,0),
+    ("layy",1,0,"v"),
+    ("ld_tap",1,1),
+    ("cd",2,0),
+    ("ld_y",3),
+    ("layy",1,3,"v"),
+    ("ld_d",3),
+    ("cd",2,1),
+    ("cd",3,0),
+    ("xy",0,0),
+    ("ld_tap",0,2),
+    ("layy",1,1,"s"),
+    ("mul",0,0),
+    ("xy",0,1),
+    ("xy",2,0),
+    ("xy",3,0),
+    ("layy",2,0,"s"),
+    ("qy",1,2),
+    ("cd",3,1),
+    ("layy",2,2,"s"),
+    ("xy",1,0),
+    ("ld_c",2,1),
+    ("xy",1,1),
+    ("xy",2,1),
+    ("layy",2,1,"s"),
+    ("mul",0,1),
+    ("xy",3,1),
+    ("turn",0,0),
+    ("ld_tap",1,2),
+    ("turn",0,1),
+    ("mul",1,0),
+    ("tout",0,2,"s"),
+    ("mul",1,1),
+    ("turn",1,0),
+    ("mul",2,0),
+    ("layy",2,3,"s"),
+    ("mul",2,1),
+    ("ld_tap",0,3),
+    ("turn",1,1),
     ("ld_ht",),
     ("cd",4,0),
-    ("cd",4,1),
-    ("widen",4,0,"s"),
-    ("xy",3,1),
-    ("tout",0,2,"v"),
-    ("xy",4,0),
-    ("layc",4,1,"s"),
-    ("xy",4,1),
-    ("cd",5,0),
-    ("turn",1,0),
-    ("turn",1,1),
-    ("mul",3,1),
-    ("turn",2,0),
-    ("turn",2,1),
-    ("xy",5,0),
-    ("widen",6,1,"s"),
-    ("cd",5,1),
-    ("xy",5,1),
-    ("qv",0,2),
-    ("mul",4,0),
-    ("layy",3,2,"s"),
     ("tout",1,2,"s"),
-    ("mul",4,1),
-    ("mul",5,0),
-    ("layy",3,1,"v"),
-    ("tout",2,2,"s"),
+    ("mul",3,0),
+    ("ld_sc","h"),
+    ("layy",3,3,"s"),
+    ("cd",4,1),
+    ("ld_c",2,0),
+    ("cd",5,0),
+    ("qy",2,2),
+    ("ld_x",2),
+    ("layy",3,2,"s"),
+    ("ld_r",),
+    ("cd",5,1),
+    ("xy",4,1),
+    ("layy",3,0,"v"),
+    ("mul",3,1),
+    ("xy",4,0),
+    ("xy",5,0),
     ("cd",6,0),
+    ("turn",2,0),
+    ("mul",4,0),
+    ("mul",4,1),
+    ("turn",2,1),
     ("turn",3,0),
     ("turn",3,1),
-    ("mul",5,1),
-    ("layy",3,0,"v"),
+    ("layy",3,1,"s"),
     ("turn",4,0),
-    ("widen",5,1,"s"),
-    ("ld_tap",0,3),
-    ("qv",1,2),
-    ("layy",3,3,"s"),
-    ("qy",3,2),
     ("turn",4,1),
-    ("layc",4,0,"v"),
-    ("widen",7,1,"s"),
-    ("cd",6,1),
-    ("cd",7,0),
-    ("layx",4,"s"),
-    ("cd",7,1),
-    ("xy",7,0),
-    ("ld_taphi",4),
-    ("layx",6,"s"),
-    ("xy",6,0),
-    ("obs",0,0),
-    ("ld_taphi",7),
-    ("obs",0,1),
-    ("layc",6,1,"v"),
-    ("widen",5,0,"s"),
-    ("tout",3,2,"s"),
-    ("xy",6,1),
-    ("layc",5,1,"s"),
-    ("xy",7,1),
-    ("qc",4,2),
+    ("tout",2,2,"s"),
+    ("qv",0,2),
+    ("xy",5,1),
     ("ld_tap",1,3),
+    ("tout",3,2,"s"),
+    ("cd",6,1),
+    ("qv",1,2),
+    ("widen",4,1,"s"),
+    ("cd",7,0),
+    ("qy",3,2),
+    ("ld_taphi",4),
+    ("mul",5,0),
+    ("mul",5,1),
+    ("xy",6,0),
+    ("ld_taphi",5),
+    ("ld_taphi",7),
+    ("xy",6,1),
     ("mul",6,0),
     ("mul",6,1),
-    ("cd",8,0),
-    ("qx",4),
-    ("cd",8,1),
-    ("xy",8,0),
-    ("tout",4,2,"s"),
-    ("turn",5,0),
-    ("qx",6),
-    ("turn",5,1),
-    ("layx",5,"s"),
-    ("qv",2,2),
-    ("turn",6,0),
-    ("mul",7,0),
     ("qv",3,2),
-    ("turn",6,1),
-    ("widen",6,0,"s"),
-    ("obs",1,0),
-    ("ld_taphi",5),
+    ("cd",7,1),
+    ("tout",4,2,"s"),
+    ("widen",4,0,"s"),
     ("qv",4,2),
-    ("tout",5,2,"s"),
+    ("qv",2,2),
+    ("ld_taphi",6),
+    ("layc",4,0,"v"),
+    ("layc",4,1,"s"),
+    ("layx",4,"s"),
+    ("qc",4,2),
+    ("qx",4),
+    ("xy",7,0),
+    ("mul",7,0),
+    ("xy",7,1),
     ("mul",7,1),
+    ("turn",5,0),
+    ("turn",5,1),
+    ("turn",6,0),
+    ("turn",6,1),
+    ("tout",5,2,"s"),
+    ("tout",6,2,"s"),
+    ("widen",5,0,"s"),
+    ("widen",5,1,"s"),
+    ("obs",0,0),
+    ("obs",0,1),
+    ("obs",0,2),
+    ("obs",1,0),
     ("obs",1,1),
     ("obs",1,2),
-    ("layc",5,0,"s"),
+    ("cd",8,0),
+    ("cd",8,1),
+    ("qv",5,2),
+    ("qv",6,2),
+    ("xy",8,0),
     ("mul",8,0),
-    ("cd",9,0),
     ("xy",8,1),
-    ("qc",5,2),
-    ("xy",9,0),
-    ("widen",7,0,"s"),
-    ("obs",0,2),
-    ("cd",9,1),
-    ("layc",7,1,"v"),
-    ("xy",9,1),
-    ("qx",5),
     ("mul",8,1),
-    ("cd",10,0),
+    ("cd",9,0),
+    ("cd",9,1),
+    ("layc",5,0,"v"),
+    ("layc",5,1,"s"),
+    ("layx",5,"s"),
+    ("qc",5,2),
+    ("qx",5),
+    ("xy",9,0),
+    ("mul",9,0),
+    ("xy",9,1),
+    ("mul",9,1),
     ("turn",7,0),
     ("turn",7,1),
-    ("tout",6,2,"s"),
     ("turn",8,0),
-    ("mul",9,0),
     ("turn",8,1),
-    ("ld_r",),
-    ("qv",6,2),
-    ("obs",0,3),
-    ("ld_taphi",6),
     ("tout",7,2,"s"),
-    ("layc",6,0,"v"),
-    ("obs",1,3),
-    ("xy",10,0),
-    ("cd",10,1),
-    ("layc",7,0,"v"),
-    ("qc",6,2),
-    ("xy",10,1),
-    ("cd",11,0),
-    ("qc",7,2),
-    ("mul",9,1),
-    ("xy",11,0),
-    ("cd",11,1),
-    ("mul",10,0),
-    ("cd",12,0),
-    ("mul",10,1),
-    ("mul",11,0),
-    ("xy",11,1),
-    ("qv",5,2),
-    ("fin",0,2),
-    ("cd",12,1),
-    ("qv",7,2),
-    ("turn",9,0),
     ("tout",8,2,"s"),
-    ("turn",9,1),
-    ("turn",10,0),
-    ("mul",11,1),
-    ("fin",1,2),
-    ("turn",10,1),
-    ("xy",12,0),
-    ("xy",12,1),
-    ("tout",9,2,"s"),
-    ("cd",13,0),
-    ("cd",13,1),
+    ("widen",6,0,"s"),
+    ("widen",6,1,"s"),
+    ("obs",0,3),
+    ("obs",1,3),
     ("obs",2,0),
     ("obs",2,1),
-    ("layx",7,"v"),
+    ("obs",2,2),
+    ("cd",10,0),
+    ("cd",10,1),
+    ("qv",7,2),
+    ("qv",8,2),
+    ("xy",10,0),
+    ("mul",10,0),
+    ("xy",10,1),
+    ("mul",10,1),
+    ("fin",0,2),
+    ("fin",1,2),
+    ("cd",11,0),
+    ("cd",11,1),
+    ("layc",6,0,"v"),
+    ("layc",6,1,"s"),
+    ("layx",6,"s"),
+    ("qc",6,2),
+    ("qx",6),
+    ("xy",11,0),
+    ("mul",11,0),
+    ("xy",11,1),
+    ("mul",11,1),
+    ("turn",9,0),
+    ("turn",9,1),
+    ("turn",10,0),
+    ("turn",10,1),
+    ("tout",9,2,"s"),
+    ("tout",10,2,"s"),
+    ("widen",7,0,"s"),
+    ("widen",7,1,"s"),
+    ("obs",2,3),
     ("obs",3,0),
-    ("tout",10,2,"v"),
-    ("qx",7),
-    ("xy",13,1),
+    ("obs",3,1),
+    ("obs",3,2),
+    ("obs",3,3),
+    ("cd",12,0),
+    ("cd",12,1),
+    ("qv",9,2),
+    ("qv",10,2),
+    ("xy",12,0),
     ("mul",12,0),
-    ("cd",14,0),
+    ("xy",12,1),
     ("mul",12,1),
+    ("fin",2,2),
+    ("fin",3,2),
+    ("cd",13,0),
+    ("cd",13,1),
+    ("layc",7,0,"v"),
+    ("layc",7,1,"s"),
+    ("layx",7,"s"),
+    ("qc",7,2),
+    ("qx",7),
+    ("xy",13,0),
+    ("mul",13,0),
+    ("xy",13,1),
+    ("mul",13,1),
     ("turn",11,0),
     ("turn",11,1),
     ("turn",12,0),
     ("turn",12,1),
-    ("xy",13,0),
-    ("qv",9,2),
-    ("obs",3,1),
-    ("obs",3,2),
-    ("qv",8,2),
-    ("cd",14,1),
     ("tout",11,2,"s"),
-    ("qv",11,2),
-    ("obs",2,2),
-    ("qv",10,2),
-    ("mul",13,0),
-    ("mul",13,1),
-    ("obs",2,3),
-    ("obs",3,3),
-    ("fin",2,2),
-    ("xy",14,0),
-    ("xy",14,1),
-    ("cd",15,0),
     ("tout",12,2,"s"),
-    ("xy",15,0),
-    ("fin",3,2),
-    ("mul",14,0),
     ("obs",4,0),
-    ("mul",14,1),
     ("obs",4,1),
-    ("cd",15,1),
     ("obs",4,2),
-    ("xy",15,1),
     ("obs",4,3),
-    ("turn",13,0),
+    ("cd",14,0),
+    ("cd",14,1),
+    ("qv",11,2),
+    ("qv",12,2),
+    ("xy",14,0),
+    ("mul",14,0),
+    ("xy",14,1),
+    ("mul",14,1),
+    ("fin",4,2),
+    ("cd",15,0),
+    ("cd",15,1),
+    ("xy",15,0),
     ("mul",15,0),
+    ("xy",15,1),
+    ("mul",15,1),
+    ("turn",13,0),
     ("turn",13,1),
     ("turn",14,0),
-    ("fin",4,2),
-    ("mul",15,1),
     ("turn",14,1),
     ("tout",13,2,"s"),
-    ("obs",5,0),
     ("tout",14,2,"s"),
-    ("qv",12,2),
+    ("obs",5,0),
     ("obs",5,1),
-    ("qv",14,2),
-    ("turn",15,0),
-    ("turn",15,1),
     ("obs",5,2),
     ("obs",5,3),
     ("qv",13,2),
-    ("obs",6,0),
+    ("qv",14,2),
+    ("turn",15,0),
+    ("turn",15,1),
     ("tout",15,2,"s"),
-    ("qv",15,2),
     ("fin",5,2),
+    ("obs",6,0),
     ("obs",6,1),
     ("obs",6,2),
     ("obs",6,3),
+    ("qv",15,2),
+    ("fin",6,2),
     ("obs",7,0),
     ("obs",7,1),
     ("obs",7,2),
     ("obs",7,3),
-    ("fin",6,2),
-    ("fin",7,2),
+    ("fin",7,0),
+    ("fin",7,1),
 ]
 
 
@@ -342,9 +347,9 @@ def tile_localised_covariance_observed_s3_kernel(
         covp = ctx.enter_context(tc.tile_pool(name="covp", bufs=4))
         grpp = ctx.enter_context(tc.tile_pool(name="grpp", bufs=3))
         resp = ctx.enter_context(tc.tile_pool(name="resp", bufs=3))
-        ps_a = ctx.enter_context(tc.psum_pool(name="ps_a", bufs=4))
-        ps_t = ctx.enter_context(tc.psum_pool(name="ps_t", bufs=2))
-        ps_o = ctx.enter_context(tc.psum_pool(name="ps_o", bufs=2))
+        ps_a = ctx.enter_context(tc.psum_pool(name="ps_a", bufs=8))
+        ps_t = ps_a
+        ps_o = ps_a
         ctx.enter_context(tc.manual_schedule())
 
         def kt(shape, dtype, name):
@@ -501,7 +506,7 @@ def tile_localised_covariance_observed_s3_kernel(
             mt, c = STEPS[s][j]
             b = 0 if mt < 2 else mt
             a = P * mt if mt < 2 else 0
-            bank = ps_a.tile([P, CH], F32, name="cov_ps")
+            bank = ps_a.tile([P, CH], F32, name="acc")
             banks[s, j] = bank
             for g in range(2):
                 nc.tensor.matmul_mx(
@@ -526,6 +531,15 @@ def tile_localised_covariance_observed_s3_kernel(
                 stop=True,
             )
 
+        warm_ps = []
+
+        def warm(n):
+            if not warm_ps:
+                warm_ps.append(ps_t.tile([P, 2, 2, P], F32, name="acc"))
+            src = c_wide[0][:, 1, 0, :]
+            for i in range(n):
+                nc.tensor.matmul(warm_ps[0][:, 0].rearrange("p u m -> p (u m)"), lhsT=src[:, 0:P], rhs=src, start=True, stop=True)
+
         cov = {}
 
         def mul(s, j):
@@ -545,7 +559,7 @@ def tile_localised_covariance_observed_s3_kernel(
 
         def turn(s, j):
             if s not in turned:
-                turned[s] = ps_t.tile([P, 2, 2, P], F32, name="turned")
+                turned[s] = ps_t.tile([P, 2, 2, P], F32, name="acc")
             for u in range(2):
                 nc.tensor.transpose(
                     turned[s][:, j, u, :], cov[s][:, j, 256 * u : 256 * (u + 1)].bitcast(F32), ident[:]
@@ -575,7 +589,7 @@ def tile_localised_covariance_observed_s3_kernel(
 
         def obs(mt, c):
             if mt not in outs:
-                outs[mt] = ps_o.tile([P, J], F32, name="out_ps")
+                outs[mt] = ps_o.tile([P, J], F32, name="acc")
             s, j = where[mt, c]
             nc.tensor.matmul_mx(
                 out=outs[mt][:],
@@ -605,7 +619,7 @@ def tile_localised_covariance_observed_s3_kernel(
             "ld_csc": ld_csc, "ld_c": ld_c, "ld_x": ld_x, "ld_sc": ld_sc, "ld_y": ld_y, "ld_d": ld_d, "ld_tap": ld_tap,
             "ld_taphi": ld_taphi, "ld_ht": ld_ht, "ld_r": ld_r, "widen": widen, "layc": layc, "layx": layx, "layy": layy,
             "qc": qc, "qx": qx, "qy": qy, "cd": cd, "xy": xy, "mul": mul, "turn": turn, "tout": tout, "qv": qv,
-            "obs": obs, "fin": fin,
+            "warm": warm, "obs": obs, "fin": fin,
         }
         for item in PROGRAM:
             calls[item[0]](*item[1:])

@@ -22,156 +22,153 @@ P = 128
 CH = 512
 NCH = N // CH
 MT = M // P
-C_CUTS = [256,256,512]
-X_CUTS = [256,256,512]
+C_CUTS = [512,512]
+X_CUTS = [512,512]
 Y_GROUPS = [[0],[1],[2],[3]]
 D_GROUPS = [[0],[1],[2],[3]]
 T_GROUPS = [[[0],[1],[2],[3]],[[0],[1],[2],[3]]]
 
 PROGRAM = [
-    ("ld_c",1,0),
-    ("ld_csc",),
-    ("widen",2,0,"v"),
     ("ld_c",0,1),
-    ("widen",3,0,"s"),
+    ("ld_csc",),
     ("ld_c",0,0),
-    ("widen",0,1,"v"),
-    ("ld_c",1,1),
-    ("layc",2,0,"s"),
-    ("ld_y",0),
     ("ld_sc","d"),
-    ("widen",0,0,"v"),
-    ("layc",0,1,"v"),
-    ("ld_d",0),
+    ("widen",0,1,"v"),
     ("widen",3,1,"s"),
-    ("widen",2,1,"s"),
+    ("widen",0,0,"v"),
+    ("ld_d",0),
+    ("layc",0,1,"v"),
+    ("ld_y",0),
     ("ld_d",1),
-    ("layy",0,0,"s"),
     ("layc",0,0,"v"),
-    ("qc",0,1),
-    ("qc",0,0),
-    ("ld_x",1),
-    ("layy",0,2,"v"),
-    ("warm",2),
-    ("layy",0,1,"v"),
-    ("layc",3,1,"v"),
-    ("layc",2,1,"s"),
-    ("layc",3,0,"s"),
     ("ld_x",0),
-    ("ld_y",1),
-    ("layy",0,3,"s"),
-    ("ld_tap",0,0),
+    ("widen",3,0,"s"),
+    ("qc",0,0),
+    ("warm",2),
+    ("qc",0,1),
+    ("layc",3,0,"v"),
+    ("layy",0,0,"v"),
+    ("widen",2,1,"s"),
+    ("layy",0,2,"v"),
     ("cd",0,0),
-    ("layx",3,"s"),
-    ("qc",2,2),
+    ("layc",3,1,"s"),
     ("qc",3,2),
-    ("layx",0,"s"),
-    ("layx",2,"v"),
-    ("qx",3),
-    ("ld_y",2),
-    ("ld_tap",0,1),
-    ("qx",2),
     ("cd",0,1),
-    ("ld_d",2),
-    ("qy",0,2),
-    ("layy",1,2,"s"),
+    ("ld_y",1),
+    ("widen",2,0,"s"),
     ("cd",1,0),
-    ("qx",0),
+    ("layc",2,1,"s"),
+    ("layy",0,3,"v"),
+    ("ld_tap",0,0),
+    ("ld_y",2),
+    ("layc",2,0,"s"),
+    ("layy",0,1,"s"),
+    ("qc",2,2),
     ("cd",1,1),
-    ("ld_tap",1,0),
-    ("layy",1,0,"v"),
-    ("ld_tap",1,1),
+    ("ld_tap",0,1),
+    ("layx",2,"v"),
+    ("layx",0,"s"),
+    ("qy",0,2),
+    ("ld_d",2),
+    ("qx",2),
     ("cd",2,0),
-    ("ld_y",3),
-    ("layy",1,3,"v"),
-    ("ld_d",3),
     ("cd",2,1),
-    ("cd",3,0),
-    ("xy",0,0),
-    ("ld_tap",0,2),
+    ("qx",0),
     ("layy",1,1,"s"),
-    ("mul",0,0),
-    ("xy",0,1),
     ("xy",2,0),
-    ("xy",3,0),
-    ("layy",2,0,"s"),
-    ("qy",1,2),
-    ("cd",3,1),
-    ("layy",2,2,"s"),
-    ("xy",1,0),
-    ("ld_c",2,1),
-    ("xy",1,1),
-    ("xy",2,1),
+    ("ld_tap",1,0),
+    ("layy",1,3,"v"),
+    ("layy",1,2,"v"),
+    ("layy",1,0,"s"),
+    ("layx",3,"s"),
+    ("ld_tap",1,1),
+    ("xy",0,0),
+    ("ld_y",3),
     ("layy",2,1,"s"),
-    ("mul",0,1),
-    ("xy",3,1),
-    ("turn",0,0),
-    ("ld_tap",1,2),
-    ("turn",0,1),
-    ("mul",1,0),
-    ("tout",0,2,"s"),
-    ("mul",1,1),
-    ("turn",1,0),
-    ("mul",2,0),
+    ("xy",0,1),
     ("layy",2,3,"s"),
-    ("mul",2,1),
+    ("ld_tap",0,2),
+    ("mul",0,0),
+    ("qy",1,2),
+    ("cd",3,0),
+    ("cd",3,1),
+    ("qx",3),
+    ("ld_c",1,0),
+    ("xy",1,0),
+    ("ld_d",3),
+    ("mul",0,1),
+    ("xy",2,1),
+    ("xy",1,1),
+    ("xy",3,0),
+    ("xy",3,1),
+    ("layy",2,2,"s"),
+    ("ld_c",1,1),
+    ("ld_tap",1,2),
+    ("mul",1,0),
+    ("mul",1,1),
     ("ld_tap",0,3),
-    ("turn",1,1),
-    ("ld_ht",),
-    ("cd",4,0),
-    ("tout",1,2,"s"),
-    ("mul",3,0),
     ("ld_sc","h"),
-    ("layy",3,3,"s"),
-    ("cd",4,1),
-    ("ld_c",2,0),
-    ("cd",5,0),
-    ("qy",2,2),
-    ("ld_x",2),
-    ("layy",3,2,"s"),
-    ("ld_r",),
-    ("cd",5,1),
-    ("xy",4,1),
-    ("layy",3,0,"v"),
-    ("mul",3,1),
-    ("xy",4,0),
-    ("xy",5,0),
-    ("cd",6,0),
+    ("ld_ht",),
+    ("turn",0,0),
+    ("layy",2,0,"s"),
+    ("ld_tap",1,3),
+    ("mul",2,0),
+    ("turn",0,1),
+    ("ld_x",1),
+    ("turn",1,0),
+    ("ld_taphi",6),
+    ("turn",1,1),
+    ("cd",4,0),
+    ("mul",2,1),
+    ("tout",0,2,"s"),
     ("turn",2,0),
-    ("mul",4,0),
-    ("mul",4,1),
+    ("qy",2,2),
+    ("tout",1,2,"s"),
+    ("ld_taphi",4),
+    ("qv",0,2),
     ("turn",2,1),
+    ("mul",3,0),
+    ("ld_taphi",7),
+    ("ld_taphi",5),
+    ("cd",4,1),
+    ("mul",3,1),
+    ("tout",2,2,"s"),
+    ("xy",4,0),
+    ("mul",4,0),
+    ("qv",1,2),
+    ("qv",2,2),
+    ("ld_r",),
+    ("xy",4,1),
+    ("mul",4,1),
+    ("cd",5,0),
+    ("cd",5,1),
+    ("layy",3,0,"v"),
+    ("layy",3,1,"s"),
+    ("layy",3,2,"s"),
+    ("layy",3,3,"s"),
+    ("widen",4,0,"s"),
+    ("widen",4,1,"s"),
+    ("qy",3,2),
+    ("xy",5,0),
+    ("mul",5,0),
+    ("xy",5,1),
+    ("mul",5,1),
     ("turn",3,0),
     ("turn",3,1),
-    ("layy",3,1,"s"),
     ("turn",4,0),
     ("turn",4,1),
-    ("tout",2,2,"s"),
-    ("qv",0,2),
-    ("xy",5,1),
-    ("ld_tap",1,3),
     ("tout",3,2,"s"),
-    ("cd",6,1),
-    ("qv",1,2),
-    ("widen",4,1,"s"),
-    ("cd",7,0),
-    ("qy",3,2),
-    ("ld_taphi",4),
-    ("mul",5,0),
-    ("mul",5,1),
-    ("xy",6,0),
-    ("ld_taphi",5),
-    ("ld_taphi",7),
-    ("xy",6,1),
-    ("mul",6,0),
-    ("mul",6,1),
-    ("qv",3,2),
-    ("cd",7,1),
     ("tout",4,2,"s"),
-    ("widen",4,0,"s"),
+    ("cd",6,0),
+    ("cd",6,1),
+    ("qv",3,2),
     ("qv",4,2),
-    ("qv",2,2),
-    ("ld_taphi",6),
+    ("xy",6,0),
+    ("mul",6,0),
+    ("xy",6,1),
+    ("mul",6,1),
+    ("cd",7,0),
+    ("cd",7,1),
     ("layc",4,0,"v"),
     ("layc",4,1,"s"),
     ("layx",4,"s"),
@@ -346,7 +343,7 @@ def tile_localised_covariance_observed_s3_kernel(
         keep = ctx.enter_context(tc.tile_pool(name="keep", bufs=1))
         covp = ctx.enter_context(tc.tile_pool(name="covp", bufs=4))
         grpp = ctx.enter_context(tc.tile_pool(name="grpp", bufs=3))
-        resp = ctx.enter_context(tc.tile_pool(name="resp", bufs=3))
+        resp = ctx.enter_context(tc.tile_pool(name="resp", bufs=6))
         ps_a = ctx.enter_context(tc.psum_pool(name="ps_a", bufs=8))
         ps_t = ps_a
         ps_o = ps_a
@@ -386,7 +383,7 @@ def tile_localised_covariance_observed_s3_kernel(
         x_lay = {b: kt([P, w, 4], BF16, f"x_lay{b}") for b, (m0, w) in BLOCKS.items()}
         y_lay = [kt([P, CH, 4], BF16, f"y_lay{c}") for c in range(NCH)]
 
-        nc.gpsimd.memset(d_sc[:].rearrange("p g n -> p (g n)").bitcast(I32), 0)
+        nc.vector.memset(d_sc[:].rearrange("p g n -> p (g n)").bitcast(I32), 0)
         nc.gpsimd.memset(ht_sc[:].rearrange("p g n -> p (g n)").bitcast(I32), 0)
         make_identity(nc, ident[:])
 

from contextlib import ExitStack

import concourse.mybir as mybir
from concourse.masks import make_identity

M, E, A, N, J = 1024, 512, 1024, 2048, 512

F32 = mybir.dt.float32
BF16 = mybir.dt.bfloat16
U32 = mybir.dt.uint32
I32 = mybir.dt.int32
U8 = mybir.dt.uint8
FP8 = mybir.dt.float8_e4m3fn
FP8X4 = mybir.dt.float8_e4m3fn_x4
FP4X4 = mybir.dt.float4_e2m1fn_x4
MULT = mybir.AluOpType.mult
COPY = mybir.ActivationFunctionType.Copy

FLOPS = 2 * M * N * (E + A + J)

P = 128
CH = 512
NCH = N // CH
MT = M // P
C_CUTS = [512,512]
X_CUTS = [512,512]
Y_GROUPS = [[0],[1],[2],[3]]
D_GROUPS = [[0],[1],[2],[3]]
T_GROUPS = [[[0],[1],[2],[3]],[[0],[1],[2],[3]]]

PROGRAM = [
    ("ld_c",0,1),
    ("ld_csc",),
    ("ld_c",0,0),
    ("ld_sc","d"),
    ("widen",0,1,"v"),
    ("widen",3,1,"s"),
    ("widen",0,0,"v"),
    ("ld_d",0),
    ("layc",0,1,"v"),
    ("ld_y",0),
    ("ld_d",1),
    ("layc",0,0,"v"),
    ("ld_x",0),
    ("widen",3,0,"s"),
    ("qc",0,0),
    ("warm",2),
    ("qc",0,1),
    ("layc",3,0,"v"),
    ("layy",0,0,"v"),
    ("widen",2,1,"s"),
    ("layy",0,2,"v"),
    ("cd",0,0),
    ("layc",3,1,"s"),
    ("qc",3,2),
    ("cd",0,1),
    ("ld_y",1),
    ("widen",2,0,"s"),
    ("cd",1,0),
    ("layc",2,1,"s"),
    ("layy",0,3,"v"),
    ("ld_tap",0,0),
    ("ld_y",2),
    ("layc",2,0,"s"),
    ("layy",0,1,"s"),
    ("qc",2,2),
    ("cd",1,1),
    ("ld_tap",0,1),
    ("layx",2,"v"),
    ("layx",0,"s"),
    ("qy",0,2),
    ("ld_d",2),
    ("qx",2),
    ("cd",2,0),
    ("cd",2,1),
    ("qx",0),
    ("layy",1,1,"s"),
    ("xy",2,0),
    ("ld_tap",1,0),
    ("layy",1,3,"v"),
    ("layy",1,2,"v"),
    ("layy",1,0,"s"),
    ("layx",3,"s"),
    ("ld_tap",1,1),
    ("xy",0,0),
    ("ld_y",3),
    ("layy",2,1,"s"),
    ("xy",0,1),
    ("layy",2,3,"s"),
    ("ld_tap",0,2),
    ("mul",0,0),
    ("qy",1,2),
    ("cd",3,0),
    ("cd",3,1),
    ("qx",3),
    ("ld_c",1,0),
    ("xy",1,0),
    ("ld_d",3),
    ("mul",0,1),
    ("xy",2,1),
    ("xy",1,1),
    ("xy",3,0),
    ("xy",3,1),
    ("layy",2,2,"s"),
    ("ld_c",1,1),
    ("ld_tap",1,2),
    ("mul",1,0),
    ("mul",1,1),
    ("ld_tap",0,3),
    ("ld_sc","h"),
    ("ld_ht",),
    ("turn",0,0),
    ("layy",2,0,"s"),
    ("ld_tap",1,3),
    ("mul",2,0),
    ("turn",0,1),
    ("ld_x",1),
    ("turn",1,0),
    ("ld_taphi",6),
    ("turn",1,1),
    ("cd",4,0),
    ("mul",2,1),
    ("tout",0,2,"s"),
    ("turn",2,0),
    ("qy",2,2),
    ("tout",1,2,"s"),
    ("ld_taphi",4),
    ("qv",0,2),
    ("turn",2,1),
    ("mul",3,0),
    ("ld_taphi",7),
    ("ld_taphi",5),
    ("cd",4,1),
    ("mul",3,1),
    ("tout",2,2,"s"),
    ("xy",4,0),
    ("mul",4,0),
    ("qv",1,2),
    ("qv",2,2),
    ("ld_r",),
    ("xy",4,1),
    ("mul",4,1),
    ("cd",5,0),
    ("cd",5,1),
    ("layy",3,0,"v"),
    ("layy",3,1,"s"),
    ("layy",3,2,"s"),
    ("layy",3,3,"s"),
    ("widen",4,0,"s"),
    ("widen",4,1,"s"),
    ("qy",3,2),
    ("xy",5,0),
    ("mul",5,0),
    ("xy",5,1),
    ("mul",5,1),
    ("turn",3,0),
    ("turn",3,1),
    ("turn",4,0),
    ("turn",4,1),
    ("tout",3,2,"s"),
    ("tout",4,2,"s"),
    ("cd",6,0),
    ("cd",6,1),
    ("qv",3,2),
    ("qv",4,2),
    ("xy",6,0),
    ("mul",6,0),
    ("xy",6,1),
    ("mul",6,1),
    ("cd",7,0),
    ("cd",7,1),
    ("layc",4,0,"v"),
    ("layc",4,1,"s"),
    ("layx",4,"s"),
    ("qc",4,2),
    ("qx",4),
    ("xy",7,0),
    ("mul",7,0),
    ("xy",7,1),
    ("mul",7,1),
    ("turn",5,0),
    ("turn",5,1),
    ("turn",6,0),
    ("turn",6,1),
    ("tout",5,2,"s"),
    ("tout",6,2,"s"),
    ("widen",5,0,"s"),
    ("widen",5,1,"s"),
    ("obs",0,0),
    ("obs",0,1),
    ("obs",0,2),
    ("obs",1,0),
    ("obs",1,1),
    ("obs",1,2),
    ("cd",8,0),
    ("cd",8,1),
    ("qv",5,2),
    ("qv",6,2),
    ("xy",8,0),
    ("mul",8,0),
    ("xy",8,1),
    ("mul",8,1),
    ("cd",9,0),
    ("cd",9,1),
    ("layc",5,0,"v"),
    ("layc",5,1,"s"),
    ("layx",5,"s"),
    ("qc",5,2),
    ("qx",5),
    ("xy",9,0),
    ("mul",9,0),
    ("xy",9,1),
    ("mul",9,1),
    ("turn",7,0),
    ("turn",7,1),
    ("turn",8,0),
    ("turn",8,1),
    ("tout",7,2,"s"),
    ("tout",8,2,"s"),
    ("widen",6,0,"s"),
    ("widen",6,1,"s"),
    ("obs",0,3),
    ("obs",1,3),
    ("obs",2,0),
    ("obs",2,1),
    ("obs",2,2),
    ("cd",10,0),
    ("cd",10,1),
    ("qv",7,2),
    ("qv",8,2),
    ("xy",10,0),
    ("mul",10,0),
    ("xy",10,1),
    ("mul",10,1),
    ("fin",0,2),
    ("fin",1,2),
    ("cd",11,0),
    ("cd",11,1),
    ("layc",6,0,"v"),
    ("layc",6,1,"s"),
    ("layx",6,"s"),
    ("qc",6,2),
    ("qx",6),
    ("xy",11,0),
    ("mul",11,0),
    ("xy",11,1),
    ("mul",11,1),
    ("turn",9,0),
    ("turn",9,1),
    ("turn",10,0),
    ("turn",10,1),
    ("tout",9,2,"s"),
    ("tout",10,2,"s"),
    ("widen",7,0,"s"),
    ("widen",7,1,"s"),
    ("obs",2,3),
    ("obs",3,0),
    ("obs",3,1),
    ("obs",3,2),
    ("obs",3,3),
    ("cd",12,0),
    ("cd",12,1),
    ("qv",9,2),
    ("qv",10,2),
    ("xy",12,0),
    ("mul",12,0),
    ("xy",12,1),
    ("mul",12,1),
    ("fin",2,2),
    ("fin",3,2),
    ("cd",13,0),
    ("cd",13,1),
    ("layc",7,0,"v"),
    ("layc",7,1,"s"),
    ("layx",7,"s"),
    ("qc",7,2),
    ("qx",7),
    ("xy",13,0),
    ("mul",13,0),
    ("xy",13,1),
    ("mul",13,1),
    ("turn",11,0),
    ("turn",11,1),
    ("turn",12,0),
    ("turn",12,1),
    ("tout",11,2,"s"),
    ("tout",12,2,"s"),
    ("obs",4,0),
    ("obs",4,1),
    ("obs",4,2),
    ("obs",4,3),
    ("cd",14,0),
    ("cd",14,1),
    ("qv",11,2),
    ("qv",12,2),
    ("xy",14,0),
    ("mul",14,0),
    ("xy",14,1),
    ("mul",14,1),
    ("fin",4,2),
    ("cd",15,0),
    ("cd",15,1),
    ("xy",15,0),
    ("mul",15,0),
    ("xy",15,1),
    ("mul",15,1),
    ("turn",13,0),
    ("turn",13,1),
    ("turn",14,0),
    ("turn",14,1),
    ("tout",13,2,"s"),
    ("tout",14,2,"s"),
    ("obs",5,0),
    ("obs",5,1),
    ("obs",5,2),
    ("obs",5,3),
    ("qv",13,2),
    ("qv",14,2),
    ("turn",15,0),
    ("turn",15,1),
    ("tout",15,2,"s"),
    ("fin",5,2),
    ("obs",6,0),
    ("obs",6,1),
    ("obs",6,2),
    ("obs",6,3),
    ("qv",15,2),
    ("fin",6,2),
    ("obs",7,0),
    ("obs",7,1),
    ("obs",7,2),
    ("obs",7,3),
    ("fin",7,0),
    ("fin",7,1),
]


def tile_localised_covariance_observed_s3_kernel(
    tc, x, y, c_bytes, c_scale, d_words, d_scales, taper, ht_words, ht_scales, r, out
):
    nc = tc.nc
    with ExitStack() as ctx:
        keep = ctx.enter_context(tc.tile_pool(name="keep", bufs=1))
        covp = ctx.enter_context(tc.tile_pool(name="covp", bufs=4))
        grpp = ctx.enter_context(tc.tile_pool(name="grpp", bufs=3))
        resp = ctx.enter_context(tc.tile_pool(name="resp", bufs=6))
        ps_a = ctx.enter_context(tc.psum_pool(name="ps_a", bufs=8))
        ps_t = ps_a
        ps_o = ps_a
        ctx.enter_context(tc.manual_schedule())

        def kt(shape, dtype, name):
            return keep.tile(shape, dtype, name=name, align_bytes=64)

        c_starts = [sum(C_CUTS[:k]) for k in range(len(C_CUTS))]
        x_starts = [sum(X_CUTS[:k]) for k in range(len(X_CUTS))]
        csc = kt([P, 2, 4], F32, "csc")
        c_in = [kt([P, 2, 4, w], U8, f"c_in{k}") for k, w in enumerate(C_CUTS)]
        x_in = [kt([P, 4, w], BF16, f"x_in{k}") for k, w in enumerate(X_CUTS)]
        y_grp = [kt([P, 4, CH * len(g)], BF16, f"y_in{k}") for k, g in enumerate(Y_GROUPS)]
        y_in = {c: y_grp[k][:, :, CH * i : CH * (i + 1)] for k, g in enumerate(Y_GROUPS) for i, c in enumerate(g)}
        d_grp = [kt([P, 2, 2 * CH * len(g)], U8, f"d_sb{k}") for k, g in enumerate(D_GROUPS)]
        d_sb = {c: d_grp[k][:, :, 2 * CH * i : 2 * CH * (i + 1)] for k, g in enumerate(D_GROUPS) for i, c in enumerate(g)}
        d_sc = kt([P, 2, N], U8, "d_sc")
        ht_sb = kt([P, 4, 2 * J], U8, "ht_sb")
        ht_sc = kt([P, 4, J], U8, "ht_sc")
        t_grp = [[kt([P, 2, CH * len(g)], BF16, f"tap_lo{b}{k}") for k, g in enumerate(T_GROUPS[b])] for b in range(2)]
        tap_lo = [{c: t_grp[b][k][:, :, CH * i : CH * (i + 1)] for k, g in enumerate(T_GROUPS[b]) for i, c in enumerate(g)} for b in range(2)]
        tap_hi = {mt: kt([P, N], BF16, f"tap_hi{mt}") for mt in range(4, MT)}
        r_sb = kt([P, J], BF16, "r_sb")
        ident = kt([P, P], F32, "ident")
        xq = kt([P, M], U32, "xq")
        xs = kt([P, M], U8, "xs")
        yq = kt([P, NCH, CH], U32, "yq")
        ys = kt([P, NCH, CH], U8, "ys")
        vq = kt([P, 16, 2 * P], U32, "vq")
        vs = kt([P, 16, 2 * P], U8, "vs")
        BLOCKS = {0: (0, 256), 2: (256, 128), 3: (384, 128), 4: (512, 128), 5: (640, 128), 6: (768, 128), 7: (896, 128)}
        cq = {b: kt([P, 2, w], U32, f"cq{b}") for b, (m0, w) in BLOCKS.items()}
        cs = {b: kt([P, 2, w], U8, f"cs{b}") for b, (m0, w) in BLOCKS.items()}
        c_wide = {b: kt([P, 2, 4, w], BF16, f"c_wide{b}") for b, (m0, w) in BLOCKS.items()}
        c_lay = {b: kt([P, 2, w, 4], BF16, f"c_lay{b}") for b, (m0, w) in BLOCKS.items()}
        x_lay = {b: kt([P, w, 4], BF16, f"x_lay{b}") for b, (m0, w) in BLOCKS.items()}
        y_lay = [kt([P, CH, 4], BF16, f"y_lay{c}") for c in range(NCH)]

        nc.vector.memset(d_sc[:].rearrange("p g n -> p (g n)").bitcast(I32), 0)
        nc.gpsimd.memset(ht_sc[:].rearrange("p g n -> p (g n)").bitcast(I32), 0)
        make_identity(nc, ident[:])

        def load(out_, in_):
            nc.sync.dma_start(out=out_, in_=in_)

        def ld_csc():
            load(csc[:], c_scale.rearrange("(g p t) o -> p g (t o)", p=P, t=4))

        def ld_c(k, g):
            m0, w = c_starts[k], C_CUTS[k]
            load(c_in[k][:, g], c_bytes[512 * g : 512 * (g + 1), m0 : m0 + w].rearrange("(p t) m -> p t m", t=4))

        def ld_x(k):
            m0, w = x_starts[k], X_CUTS[k]
            load(x_in[k][:], x[:, m0 : m0 + w].rearrange("(p t) m -> p t m", t=4))

        def ld_sc(which):
            dst, src = (d_sc, d_scales) if which == "d" else (ht_sc, ht_scales)
            for q in range(4):
                load(
                    dst[32 * q : 32 * q + 4].bitcast(I32),
                    src[:, 4 * q : 4 * q + 4, :].rearrange("g q n -> q g n").bitcast(I32),
                )

        def ld_y(k):
            n0, w = CH * Y_GROUPS[k][0], CH * len(Y_GROUPS[k])
            load(y_grp[k][:], y[:, n0 : n0 + w].rearrange("(p t) n -> p t n", t=4))

        def ld_d(k):
            n0, w = 2 * CH * D_GROUPS[k][0], 2 * CH * len(D_GROUPS[k])
            load(d_grp[k][:], d_words[:, :, n0 : n0 + w].rearrange("g p b -> p g b"))

        def ld_tap(b, k):
            n0, w = CH * T_GROUPS[b][k][0], CH * len(T_GROUPS[b][k])
            load(t_grp[b][k][:], taper[256 * b : 256 * (b + 1), n0 : n0 + w].rearrange("(j m) n -> m j n", j=2))

        def ld_taphi(mt):
            load(tap_hi[mt][:], taper[P * mt : P * (mt + 1), :])

        def ld_ht():
            load(ht_sb[:], ht_words.rearrange("g p b -> p g b"))

        def ld_r():
            load(r_sb[:], r.partition_broadcast(P))

        def cut(starts, m0):
            k = max(i for i in range(len(starts)) if starts[i] <= m0)
            return k, m0 - starts[k]

        def lay(eng, dst, src):
            d = dst.rearrange("p (c i) t -> p c t i", i=4)
            s = src.rearrange("p t (c i) -> p c t i", i=4)
            if eng == "v":
                nc.vector.tensor_copy(out=d, in_=s)
            else:
                nc.scalar.copy(out=d, in_=s)

        def quant(codes, scales, src):
            nc.vector.quantize_mx(out=codes.bitcast(FP8X4), scales=scales, in_=src)

        def widen(b, g, eng):
            m0, w = BLOCKS[b]
            k, a = cut(c_starts, m0)
            for t in range(4):
                i_ = c_in[k][:, g, t, a : a + w].bitcast(FP8)
                s_ = csc[:, g, t : t + 1]
                o_ = c_wide[b][:, g, t, :]
                if eng == "v":
                    nc.vector.tensor_scalar(out=o_, in0=i_, scalar1=s_, scalar2=None, op0=MULT)
                else:
                    nc.scalar.activation(out=o_, in_=i_, func=COPY, scale=s_)

        def layc(b, g, eng):
            lay(eng, c_lay[b][:, g], c_wide[b][:, g])

        def layx(b, eng):
            m0, w = BLOCKS[b]
            k, a = cut(x_starts, m0)
            lay(eng, x_lay[b][:], x_in[k][:, :, a : a + w])

        def layy(c, i, eng):
            lay(eng, y_lay[c][:, 128 * i : 128 * (i + 1), :], y_in[c][:, :, 128 * i : 128 * (i + 1)])

        def qc(b, g):
            if g < 2:
                quant(cq[b][:, g, :], cs[b][:, g, :], c_lay[b][:, g].rearrange("p m t -> p (m t)"))
            else:
                quant(
                    cq[b][:].rearrange("p g m -> p (g m)"),
                    cs[b][:].rearrange("p g m -> p (g m)"),
                    c_lay[b][:].rearrange("p g m t -> p (g m t)"),
                )

        def qx(b):
            m0, w = BLOCKS[b]
            quant(xq[:, m0 : m0 + w], xs[:, m0 : m0 + w], x_lay[b][:].rearrange("p m t -> p (m t)"))

        def qy(c, half):
            if half < 2:
                n0 = 256 * half
                quant(yq[:, c, n0 : n0 + 256], ys[:, c, n0 : n0 + 256], y_lay[c][:, n0 : n0 + 256].rearrange("p n t -> p (n t)"))
            else:
                quant(yq[:, c, :], ys[:, c, :], y_lay[c][:].rearrange("p n t -> p (n t)"))

        STEPS = [[(0, 0), (1, 0)], [(0, 1), (1, 1)], [(2, 0), (2, 1)], [(3, 0), (3, 1)], [(0, 2), (1, 2)], [(2, 2), (3, 2)], [(0, 3), (1, 3)], [(2, 3), (3, 3)]]
        for mt in range(4, MT):
            STEPS += [[(mt, 0), (mt, 1)], [(mt, 2), (mt, 3)]]
        where = {}
        for s, units in enumerate(STEPS):
            for j, u in enumerate(units):
                where[u] = (s, j)

        banks = {}

        def cd(s, j):
            mt, c = STEPS[s][j]
            b = 0 if mt < 2 else mt
            a = P * mt if mt < 2 else 0
            bank = ps_a.tile([P, CH], F32, name="acc")
            banks[s, j] = bank
            for g in range(2):
                nc.tensor.matmul_mx(
                    out=bank[:],
                    lhsT=cq[b][:, g, a : a + P].bitcast(FP8X4),
                    lhsT_scale=cs[b][:, g, a : a + P],
                    rhs=d_sb[c][:, g, :].bitcast(FP4X4),
                    rhs_scale=d_sc[:, g, CH * c : CH * (c + 1)],
                    start=(g == 0),
                    stop=False,
                )

        def xy(s, j):
            mt, c = STEPS[s][j]
            nc.tensor.matmul_mx(
                out=banks[s, j][:],
                lhsT=xq[:, P * mt : P * (mt + 1)].bitcast(FP8X4),
                lhsT_scale=xs[:, P * mt : P * (mt + 1)],
                rhs=yq[:, c, :].bitcast(FP8X4),
                rhs_scale=ys[:, c, :],
                start=False,
                stop=True,
            )

        warm_ps = []

        def warm(n):
            if not warm_ps:
                warm_ps.append(ps_t.tile([P, 2, 2, P], F32, name="acc"))
            src = c_wide[0][:, 1, 0, :]
            for i in range(n):
                nc.tensor.matmul(warm_ps[0][:, 0].rearrange("p u m -> p (u m)"), lhsT=src[:, 0:P], rhs=src, start=True, stop=True)

        cov = {}

        def mul(s, j):
            mt, c = STEPS[s][j]
            if s not in cov:
                cov[s] = covp.tile([P, 2, CH], BF16, name="cov", align_bytes=64)
            tp_ = tap_lo[mt // 2][c][:, mt % 2, :] if mt < 4 else tap_hi[mt][:, CH * c : CH * (c + 1)]
            nc.vector.tensor_tensor(
                out=cov[s][:, j, :].rearrange("m (u p e) -> m u p e", u=2, e=2),
                in0=banks[s, j][:].rearrange("m (p u e) -> m u p e", u=2, e=2),
                in1=tp_.rearrange("m (p u e) -> m u p e", u=2, e=2),
                op=MULT,
            )

        turned = {}
        grp = {}

        def turn(s, j):
            if s not in turned:
                turned[s] = ps_t.tile([P, 2, 2, P], F32, name="acc")
            for u in range(2):
                nc.tensor.transpose(
                    turned[s][:, j, u, :], cov[s][:, j, 256 * u : 256 * (u + 1)].bitcast(F32), ident[:]
                )

        def tout(s, j, eng):
            if s not in grp:
                grp[s] = grpp.tile([P, 2, P, 4], BF16, name="grp", align_bytes=64)
            if j < 2:
                o_ = grp[s][:, j].rearrange("p m t -> p (m t)").bitcast(F32).rearrange("p (m u) -> p m u", u=2)
                i_ = turned[s][:, j].rearrange("p u m -> p m u")
            else:
                o_ = grp[s][:].rearrange("p j m t -> p (j m t)").bitcast(F32).rearrange("p (j m u) -> p j m u", j=2, u=2)
                i_ = turned[s][:].rearrange("p j u m -> p j m u")
            if eng == "v":
                nc.vector.tensor_copy(out=o_, in_=i_)
            else:
                nc.scalar.copy(out=o_, in_=i_)

        def qv(s, j):
            if j < 2:
                quant(vq[:, s, P * j : P * (j + 1)], vs[:, s, P * j : P * (j + 1)], grp[s][:, j].rearrange("p m t -> p (m t)"))
            else:
                quant(vq[:, s, :], vs[:, s, :], grp[s][:].rearrange("p j m t -> p (j m t)"))

        outs = {}

        def obs(mt, c):
            if mt not in outs:
                outs[mt] = ps_o.tile([P, J], F32, name="acc")
            s, j = where[mt, c]
            nc.tensor.matmul_mx(
                out=outs[mt][:],
                lhsT=vq[:, s, P * j : P * (j + 1)].bitcast(FP8X4),
                lhsT_scale=vs[:, s, P * j : P * (j + 1)],
                rhs=ht_sb[:, c, :].bitcast(FP4X4),
                rhs_scale=ht_sc[:, c, :],
                start=(c == 0),
                stop=(c == NCH - 1),
            )

        res = {}

        def fin(mt, h):
            if h == 2:
                res[mt] = resp.tile([P, J], F32, name="res", align_bytes=64)
                nc.vector.tensor_tensor(out=res[mt][:], in0=outs[mt][:], in1=r_sb[:], op=MULT)
                nc.sync.dma_start(out=out[P * mt : P * (mt + 1), :], in_=res[mt][:])
            else:
                if mt not in res:
                    res[mt] = resp.tile([P, J], F32, name="res", align_bytes=64)
                cols = slice(256 * h, 256 * (h + 1))
                nc.vector.tensor_tensor(out=res[mt][:, cols], in0=outs[mt][:, cols], in1=r_sb[:, cols], op=MULT)
                nc.sync.dma_start(out=out[P * mt : P * (mt + 1), cols], in_=res[mt][:, cols])

        calls = {
            "ld_csc": ld_csc, "ld_c": ld_c, "ld_x": ld_x, "ld_sc": ld_sc, "ld_y": ld_y, "ld_d": ld_d, "ld_tap": ld_tap,
            "ld_taphi": ld_taphi, "ld_ht": ld_ht, "ld_r": ld_r, "widen": widen, "layc": layc, "layx": layx, "layy": layy,
            "qc": qc, "qx": qx, "qy": qy, "cd": cd, "xy": xy, "mul": mul, "turn": turn, "tout": tout, "qv": qv,
            "warm": warm, "obs": obs, "fin": fin,
        }
        for item in PROGRAM:
            calls[item[0]](*item[1:])
